import numpy as np
import ml_dtypes


def mxq(x, axis, fmt="e4m3"):
    dtype, down = {"e4m3": (ml_dtypes.float8_e4m3fn, 7), "e5m2": (ml_dtypes.float8_e5m2, 14)}[fmt]
    v = np.moveaxis(np.asarray(x, np.float32).astype(ml_dtypes.bfloat16).astype(np.float64), axis, -1)
    blocks = v.reshape(v.shape[:-1] + (-1, 32))
    amax = np.abs(blocks).max(-1, keepdims=True)
    byte = np.maximum(np.where(amax > 0, np.frexp(amax)[1] - 1 + 127, 0) - down, 1)
    scale = np.exp2(byte - 127.0)
    codes = (blocks / scale).astype(np.float32).astype(dtype).astype(np.float64)
    return np.moveaxis((codes * scale).reshape(v.shape), -1, axis)


WIDE = False


def mx_kscale(k):
    if not WIDE:
        return np.ones(k)
    levels = np.array([24, -24, 12, -12, 0])
    if k % 512:
        return np.exp2(np.random.permutation(np.resize(levels, k // 32))).repeat(32)
    a = np.empty((k // 512, 16))
    for p in range(k // 512):
        a[p, :8] = np.random.permutation(np.resize(levels, 8))
        for g in range(8):
            far = levels[np.abs(levels - a[p, g]) >= 10]
            a[p, g + 8] = far[np.random.randint(len(far))]
    return np.exp2(a.ravel()).repeat(32)


def f64(x):
    return np.asarray(x).astype(np.float64)


def striped(idx):
    return np.tile(idx.reshape(-1, 16).T, (8, 1)).astype(np.uint16)


def unstriped(offs):
    return offs[:16].T.reshape(-1).astype(np.int64)


E2M1 = np.array([0.0, 0.5, 1.0, 1.5, 2.0, 3.0, 4.0, 6.0, -0.0, -0.5, -1.0, -1.5, -2.0, -3.0, -4.0, -6.0])


def pack_weight(w, fmt):
    k, n = w.shape
    w = f64(np.asarray(w, np.float32).astype(ml_dtypes.bfloat16)).reshape(k // 32, 32, n)
    amax = np.abs(w).max(1)
    if fmt == "e4m3":
        byte = np.frexp(amax)[1] - 1 + 127 - 7
    else:
        mant, ex = np.frexp(amax / 6.0)
        byte = np.where(mant > 0.5, ex, ex - 1) + 127
    byte = np.clip(np.where(amax > 0, byte, 1), 1, 254)
    scaled = (w * np.exp2(127.0 - byte)[:, None, :]).reshape(k, n).astype(np.float32)
    by_word = np.ascontiguousarray(scaled.reshape(k // 512, 128, 4, n).transpose(0, 1, 3, 2))
    if fmt == "e4m3":
        words = by_word.astype(ml_dtypes.float8_e4m3fn).view(np.uint8)
    else:
        c = by_word.astype(ml_dtypes.float4_e2m1fn).view(np.uint8) & 0xF
        words = (c[..., 0::2] | (c[..., 1::2] << 4)).reshape(k // 512, 128, 2 * n)
    return np.ascontiguousarray(words), np.ascontiguousarray(byte.astype(np.uint8).reshape(k // 512, 16, n))


def unpack_weight(words, scales, fmt):
    g, _, n = scales.shape
    words = np.ascontiguousarray(words).reshape(g, 128, n, -1)
    if fmt == "e4m3":
        vals = words.view(ml_dtypes.float8_e4m3fn).astype(np.float64)
    else:
        nib = np.empty((g, 128, n, 4), np.uint8)
        nib[..., 0::2] = words & 0xF
        nib[..., 1::2] = words >> 4
        vals = E2M1[nib]
    vals = vals * np.repeat(np.exp2(scales.astype(np.float64) - 127.0), 8, axis=1)[..., None]
    return vals.transpose(0, 1, 3, 2).reshape(g * 512, n)


K, L, N, T, J = 1024, 512, 512, 2048, 1024


def setup_inputs():
    n = np.random.standard_normal
    s = mx_kscale(K)[:, None]
    s2 = mx_kscale(L)[:, None]
    p_tab = pack_weight(n((K, T)) * s, "e4m3")
    p_wx = pack_weight(n((L, N)) / np.sqrt(L) / s2, "e2m1")
    return {
        "tab_words": p_tab[0],
        "tab_scales": p_tab[1],
        "wt": (n((K, N)) / np.sqrt(K) / s).astype(np.float32),
        "x": (n((L, J)) * s2).astype(np.float32),
        "wx_words": p_wx[0],
        "wx_scales": p_wx[1],
        "offs": striped(np.random.permutation(T)[:J]),
    }


def reference(tab_words, tab_scales, wt, x, wx_words, wx_scales, offs):
    idx = unstriped(offs)
    tab_ = unpack_weight(tab_words, tab_scales, "e4m3")[:, idx]
    wt_q_ = mxq(f64(wt), 0, "e4m3")
    wt_r_ = mxq(f64(wt) - wt_q_, 0, "e4m3")
    x_ = mxq(f64(x), 0, "e4m3")
    wx_ = unpack_weight(wx_words, wx_scales, "e2m1")
    y = wt_q_.T @ tab_ + wt_r_.T @ tab_ + wx_.T @ x_
    return y

@@ -1,0 +1,273 @@
+from contextlib import ExitStack
+
+import concourse.mybir as mybir
+from concourse.masks import make_identity
+
+K, L, N, T, J = 1024, 512, 512, 2048, 1024
+FLOPS = 3221225472
+
+F32 = mybir.dt.float32
+BF16 = mybir.dt.bfloat16
+I32 = mybir.dt.int32
+U32 = mybir.dt.uint32
+U16 = mybir.dt.uint16
+U8 = mybir.dt.uint8
+FP8X4 = mybir.dt.float8_e4m3fn_x4
+FP4X4 = mybir.dt.float4_e2m1fn_x4
+SUB = mybir.AluOpType.subtract
+
+P = 128
+PACK = 4
+KP = P * PACK
+JH = 512
+JQ = 256
+NH = 256
+NC = 128
+LATE = ((2, 1), (3, 1),)
+ON_VECTOR = ((3, 1), )
+PLACED = {"eye": 0, "plane0": 0, "wq00_plane": 512, "wq01_plane": 768, "words00": 1024, "wq10_plane": 3072, "wq11_plane": 3328, "xq0_plane": 3584}
+SHARE = {"words01": "w_raw00", "plane1": "w_bf00"}
+
+
+def woven(ap):
+    return ap.rearrange("p (c i) t -> p c t i", i=4)
+
+
+def by_rows(ap):
+    return ap.rearrange("p t (c i) -> p c t i", i=4)
+
+
+def tile_list_tiert_none_kernel(tc, tab_words, tab_scales, wt, x, wx_words, wx_scales, offs, out):
+    nc = tc.nc
+    with ExitStack() as ctx:
+        keep = ctx.enter_context(tc.tile_pool(name="keep", bufs=1))
+        reuse = ctx.enter_context(tc.tile_pool(name="reuse", bufs=1))
+        psum = ctx.enter_context(tc.psum_pool(name="psum", bufs=1))
+
+        def sb(shape, dtype, name):
+            if name in PLACED:
+                return reuse.tile(shape, dtype, name=name, align_bytes=64, offset=PLACED[name])
+            return keep.tile(shape, dtype, name=name, tag=SHARE.get(name, name), align_bytes=64)
+
+        offsets = keep.tile([P, J // 16], U16, name="offsets")
+        tab_plane = sb([P, T], U8, "tab_plane")
+        wx_plane = sb([P, N], U8, "wx_plane")
+        wx_codes = sb([P, 2 * N], U8, "wx_codes")
+        ident = sb([P, P], BF16, "ident")
+        eye = sb([P, 4 * 513 + 12], BF16, "eye")
+        eye_codes = sb([P, KP], U32, "eye_codes")
+        eye_plane = sb([P, KP], U8, "eye_plane")
+        w_raw, tab_raw, x_raw = {}, {}, {}
+        planes, words, wq, wr, xq, acc, back, r_bf = {}, {}, {}, {}, {}, {}, {}, {}
+        done = {}
+
+        def load_offs():
+            nc.sync.dma_start(offsets[:], offs)
+
+        def load_ts(eng, q):
+            eng.dma_start(tab_plane[32 * q : 32 * q + 8, :].bitcast(I32), tab_scales[:, 4 * q : 4 * q + 4, :].bitcast(I32))
+
+        def load_ws(eng, q):
+            eng.dma_start(wx_plane[32 * q : 32 * q + 4, :].bitcast(I32), wx_scales[0, 4 * q : 4 * q + 4, :].bitcast(I32))
+
+        def load_wxw(eng):
+            eng.dma_start(wx_codes[:].bitcast(I32), wx_words[0].bitcast(I32))
+
+        def load_w(eng, a, u):
+            w_raw[a, u] = sb([P, PACK, NH], F32, f"w_raw{a}{u}")
+            eng.dma_start(w_raw[a, u][:], wt[KP * a : KP * (a + 1), NH * u : NH * (u + 1)].rearrange("(p j) n -> p j n", j=PACK))
+
+        def load_tab(eng, a):
+            tab_raw[a] = sb([P, T], I32, f"tab_raw{a}")
+            eng.dma_start(tab_raw[a][:], tab_words[a].rearrange("p t i -> p (t i)").bitcast(I32))
+
+        def load_x(eng, h, s):
+            x_raw[h, s] = sb([P, PACK, JQ], F32, f"x_raw{h}{s}")
+            j0 = JH * h + JQ * s
+            eng.dma_start(x_raw[h, s][:], x[:, j0 : j0 + JQ].rearrange("(p j) w -> p j w", j=PACK))
+
+        def make_eye():
+            make_identity(nc, ident[:])
+            nc.vector.memset(eye[:].bitcast(I32), 0)
+            nc.vector.tensor_copy(
+                out=eye[:, 0 : 4 * 513].rearrange("p (j m) -> p j m", j=4)[:, :, 0:512:4],
+                in_=ident[:].unsqueeze(1).to_broadcast([P, 4, P]),
+            )
+            nc.vector.quantize_mx(out=eye_codes[:].bitcast(FP8X4), scales=eye_plane[:], in_=eye[:, 0 : 4 * KP])
+
+        def gather_plane(h):
+            planes[h] = sb([P, JH], U8, f"plane{h}")
+            nc.vector.tensor_copy(planes[h][:], tab_plane[:].indirect(offsets[:, 32 * h : 32 * (h + 1)]))
+
+        def gather_words(a, h):
+            words[a, h] = sb([P, JH], U32, f"words{a}{h}")
+            nc.vector.tensor_copy(words[a, h][:], tab_raw[a][:].bitcast(U32).indirect(offsets[:, 32 * h : 32 * (h + 1)]))
+
+        def quantize(grouped, width, name):
+            codes = sb([P, width], U32, name + "_codes")
+            plane = sb([P, width], U8, name + "_plane")
+            nc.vector.quantize_mx(out=codes[:].bitcast(FP8X4), scales=plane[:], in_=grouped[:].rearrange("p w t -> p (w t)"))
+            return codes, plane
+
+        def first_tier(a, u):
+            grouped = sb([P, NH, PACK], BF16, f"w_bf{a}{u}")
+            nc.scalar.copy(out=woven(grouped[:]), in_=by_rows(w_raw[a, u][:]))
+            wq[a, u] = quantize(grouped, NH, f"wq{a}{u}")
+
+        def read_back(a, u, v):
+            codes, plane = wq[a, u]
+            cols = slice(NC * v, NC * (v + 1))
+            back[a, u, v] = psum.tile([P, PACK, NC], F32, name="back", tag="shared", bufs=2)
+            for t in range(PACK):
+                nc.tensor.matmul_mx(
+                    out=back[a, u, v][:, t, :],
+                    lhsT=eye_codes[:, P * t : P * (t + 1)].bitcast(FP8X4),
+                    lhsT_scale=eye_plane[:, P * t : P * (t + 1)],
+                    rhs=codes[:, cols].bitcast(FP8X4),
+                    rhs_scale=plane[:, cols],
+                    start=True,
+                    stop=True,
+                )
+
+        def leftover(a, u, v):
+            cols = slice(NC * v, NC * (v + 1))
+            if (a, u) not in r_bf:
+                r_bf[a, u] = sb([P, NH, PACK], BF16, f"r_bf{a}{u}")
+            nc.vector.tensor_tensor(out=woven(r_bf[a, u][:, cols, :]), in0=by_rows(w_raw[a, u][:, :, cols]), in1=by_rows(back[a, u, v][:]), op=SUB)
+
+        def second_tier(a, u):
+            wr[a, u] = quantize(r_bf[a, u], NH, f"wr{a}{u}")
+
+        def quantize_x(h, s):
+            if h not in xq:
+                xq[h] = (sb([P, JH], U32, f"xq{h}_codes"), sb([P, JH], U8, f"xq{h}_plane"))
+            codes, plane = xq[h]
+            cols = slice(JQ * s, JQ * (s + 1))
+            grouped = sb([P, JQ, PACK], BF16, f"x_bf{h}{s}")
+            nc.scalar.copy(out=woven(grouped[:]), in_=by_rows(x_raw[h, s][:]))
+            nc.vector.quantize_mx(out=codes[:, cols].bitcast(FP8X4), scales=plane[:, cols], in_=grouped[:].rearrange("p w t -> p (w t)"))
+
+        def add_pass(c, h, lhsT, lhsT_scale, rhs, rhs_scale):
+            count = done.get((c, h), 0)
+            if count == 0:
+                if (c, h) in LATE:
+                    acc[c, h] = psum.tile([P, JH], F32, name="late", tag="shared", bufs=2)
+                else:
+                    acc[c, h] = psum.tile([P, JH], F32, name=f"acc{c}{h}")
+            nc.tensor.matmul_mx(out=acc[c, h][:], lhsT=lhsT, lhsT_scale=lhsT_scale, rhs=rhs, rhs_scale=rhs_scale, start=(count == 0), stop=(count == 4))
+            done[c, h] = count + 1
+            if count == 4:
+                pieces = 1
+                width = JH // pieces
+                for piece in range(pieces):
+                    cols = slice(width * piece, width * (piece + 1))
+                    res = sb([P, width], F32, f"res{c}{h}{piece}")
+                    if (c, h) in ON_VECTOR:
+                        nc.vector.tensor_copy(out=res[:], in_=acc[c, h][:, cols])
+                    else:
+                        nc.scalar.copy(out=res[:], in_=acc[c, h][:, cols])
+                    j0 = JH * h + width * piece
+                    nc.sync.dma_start(out[NC * c : NC * (c + 1), j0 : j0 + width], res[:])
+
+        def tab_pass(tier, a, c, h):
+            codes, plane = tier[a, c // 2]
+            cols = slice(NC * (c % 2), NC * (c % 2 + 1))
+            add_pass(c, h, codes[:, cols].bitcast(FP8X4), plane[:, cols], words[a, h][:].bitcast(FP8X4), planes[h][4 * a : P, :])
+
+        def x_pass(c, h):
+            codes, plane = xq[h]
+            add_pass(c, h, wx_codes[:, 2 * NC * c : 2 * NC * (c + 1)].bitcast(FP4X4), wx_plane[:, NC * c : NC * (c + 1)], codes[:].bitcast(FP8X4), plane[:])
+
+        nc.gpsimd.memset(tab_plane[:].bitcast(I32), 0)
+        load_offs()
+        load_w(nc.sync, 0, 0)
+        for q in range(4):
+            load_ts(nc.sync, q)
+        make_eye()
+        nc.gpsimd.memset(wx_plane[:].bitcast(I32), 0)
+        load_w(nc.sync, 0, 1)
+        load_tab(nc.sync, 0)
+        load_wxw(nc.sync)
+        load_w(nc.sync, 1, 0)
+        for q in range(4):
+            load_ws(nc.sync, q)
+        load_w(nc.sync, 1, 1)
+        load_x(nc.sync, 0, 0)
+        load_x(nc.sync, 0, 1)
+        load_x(nc.sync, 1, 0)
+        load_x(nc.sync, 1, 1)
+        load_tab(nc.sync, 1)
+        gather_plane(0)
+        first_tier(0, 0)
+        read_back(0, 0, 0)
+        read_back(0, 0, 1)
+        gather_plane(1)
+        first_tier(0, 1)
+        leftover(0, 0, 0)
+        read_back(0, 1, 0)
+        leftover(0, 0, 1)
+        read_back(0, 1, 1)
+        gather_words(0, 0)
+        tab_pass(wq, 0, 0, 0)
+        tab_pass(wq, 0, 1, 0)
+        tab_pass(wq, 0, 2, 0)
+        tab_pass(wq, 0, 3, 0)
+        second_tier(0, 0)
+        tab_pass(wr, 0, 0, 0)
+        tab_pass(wr, 0, 1, 0)
+        gather_words(0, 1)
+        tab_pass(wq, 0, 0, 1)
+        tab_pass(wr, 0, 0, 1)
+        tab_pass(wq, 0, 1, 1)
+        tab_pass(wr, 0, 1, 1)
+        leftover(0, 1, 0)
+        leftover(0, 1, 1)
+        first_tier(1, 0)
+        read_back(1, 0, 0)
+        read_back(1, 0, 1)
+        second_tier(0, 1)
+        tab_pass(wr, 0, 2, 0)
+        tab_pass(wr, 0, 3, 0)
+        first_tier(1, 1)
+        leftover(1, 0, 0)
+        read_back(1, 1, 0)
+        leftover(1, 0, 1)
+        read_back(1, 1, 1)
+        quantize_x(0, 0)
+        quantize_x(0, 1)
+        x_pass(0, 0)
+        x_pass(1, 0)
+        x_pass(2, 0)
+        x_pass(3, 0)
+        second_tier(1, 0)
+        leftover(1, 1, 0)
+        tab_pass(wq, 0, 2, 1)
+        tab_pass(wr, 0, 2, 1)
+        leftover(1, 1, 1)
+        tab_pass(wq, 0, 3, 1)
+        tab_pass(wr, 0, 3, 1)
+        quantize_x(1, 0)
+        second_tier(1, 1)
+        quantize_x(1, 1)
+        x_pass(0, 1)
+        x_pass(1, 1)
+        x_pass(2, 1)
+        x_pass(3, 1)
+        gather_words(1, 0)
+        tab_pass(wq, 1, 0, 0)
+        tab_pass(wr, 1, 0, 0)
+        tab_pass(wq, 1, 1, 0)
+        tab_pass(wr, 1, 1, 0)
+        tab_pass(wq, 1, 2, 0)
+        tab_pass(wr, 1, 2, 0)
+        tab_pass(wq, 1, 3, 0)
+        tab_pass(wr, 1, 3, 0)
+        gather_words(1, 1)
+        tab_pass(wq, 1, 0, 1)
+        tab_pass(wr, 1, 0, 1)
+        tab_pass(wq, 1, 1, 1)
+        tab_pass(wr, 1, 1, 1)
+        tab_pass(wq, 1, 2, 1)
+        tab_pass(wr, 1, 2, 1)
+        tab_pass(wq, 1, 3, 1)
+        tab_pass(wr, 1, 3, 1)

@@ -25,8 +25,8 @@ NH = 256
 NC = 128
 LATE = ((2, 1), (3, 1),)
 ON_VECTOR = ((3, 1), )
-PLACED = {"eye": 0, "plane0": 0, "wq00_plane": 512, "wq01_plane": 768, "words00": 1024, "wq10_plane": 3072, "wq11_plane": 3328, "xq0_plane": 3584}
-SHARE = {"words01": "w_raw00", "plane1": "w_bf00"}
+PLACED = {"eye": 0, "plane0": 0, "wq00_plane": 512, "wq01_plane": 768, "words00": 1024, "wq10_plane": 3072, "wq11_plane": 3328, "xq0_plane": 3584, "x_raw1": 4160, "res000": 4160, "res100": 6208, "res200": 8256, "res300": 10304}
+SHARE = {"words01": "w_raw00", "plane1": "w_bf00", "words10": "w_bf01", "words11": "x_bf11"}
 
 
 def woven(ap):
@@ -76,6 +76,18 @@ def tile_list_tiert_none_kernel(tc, tab_words, tab_scales, wt, x, wx_words, wx_s
         def load_w(eng, a, u):
             w_raw[a, u] = sb([P, PACK, NH], F32, f"w_raw{a}{u}")
             eng.dma_start(w_raw[a, u][:], wt[KP * a : KP * (a + 1), NH * u : NH * (u + 1)].rearrange("(p j) n -> p j n", j=PACK))
+
+        def load_w_pass(eng, a):
+            whole = sb([P, PACK, N], F32, f"w_raw{a}")
+            eng.dma_start(whole[:], wt[KP * a : KP * (a + 1), :].rearrange("(p j) n -> p j n", j=PACK))
+            for u in range(2):
+                w_raw[a, u] = whole[:, :, NH * u : NH * (u + 1)]
+
+        def load_x_half(eng, h):
+            half = sb([P, PACK, JH], F32, f"x_raw{h}")
+            eng.dma_start(half[:], x[:, JH * h : JH * (h + 1)].rearrange("(p j) w -> p j w", j=PACK))
+            for s in range(2):
+                x_raw[h, s] = half[:, :, JQ * s : JQ * (s + 1)]
 
         def load_tab(eng, a):
             tab_raw[a] = sb([P, T], I32, f"tab_raw{a}")
@@ -157,7 +169,7 @@ def tile_list_tiert_none_kernel(tc, tab_words, tab_scales, wt, x, wx_words, wx_s
             nc.tensor.matmul_mx(out=acc[c, h][:], lhsT=lhsT, lhsT_scale=lhsT_scale, rhs=rhs, rhs_scale=rhs_scale, start=(count == 0), stop=(count == 4))
             done[c, h] = count + 1
             if count == 4:
-                pieces = 1
+                pieces = 2 if (c, h) == (3, 1) else 1
                 width = JH // pieces
                 for piece in range(pieces):
                     cols = slice(width * piece, width * (piece + 1))
@@ -185,31 +197,28 @@ def tile_list_tiert_none_kernel(tc, tab_words, tab_scales, wt, x, wx_words, wx_s
             load_ts(nc.sync, q)
         make_eye()
         nc.gpsimd.memset(wx_plane[:].bitcast(I32), 0)
-        load_w(nc.sync, 0, 1)
         load_tab(nc.sync, 0)
+        load_w(nc.sync, 0, 1)
         load_wxw(nc.sync)
-        load_w(nc.sync, 1, 0)
+        load_tab(nc.sync, 1)
         for q in range(4):
             load_ws(nc.sync, q)
-        load_w(nc.sync, 1, 1)
-        load_x(nc.sync, 0, 0)
-        load_x(nc.sync, 0, 1)
-        load_x(nc.sync, 1, 0)
-        load_x(nc.sync, 1, 1)
-        load_tab(nc.sync, 1)
+        load_w_pass(nc.sync, 1)
+        load_x_half(nc.sync, 0)
+        load_x_half(nc.sync, 1)
         gather_plane(0)
         first_tier(0, 0)
         read_back(0, 0, 0)
         read_back(0, 0, 1)
         gather_plane(1)
-        first_tier(0, 1)
-        leftover(0, 0, 0)
-        read_back(0, 1, 0)
-        leftover(0, 0, 1)
-        read_back(0, 1, 1)
         gather_words(0, 0)
         tab_pass(wq, 0, 0, 0)
         tab_pass(wq, 0, 1, 0)
+        leftover(0, 0, 0)
+        leftover(0, 0, 1)
+        first_tier(0, 1)
+        read_back(0, 1, 0)
+        read_back(0, 1, 1)
         tab_pass(wq, 0, 2, 0)
         tab_pass(wq, 0, 3, 0)
         second_tier(0, 0)
@@ -222,46 +231,46 @@ def tile_list_tiert_none_kernel(tc, tab_words, tab_scales, wt, x, wx_words, wx_s
         tab_pass(wr, 0, 1, 1)
         leftover(0, 1, 0)
         leftover(0, 1, 1)
-        first_tier(1, 0)
-        read_back(1, 0, 0)
-        read_back(1, 0, 1)
         second_tier(0, 1)
         tab_pass(wr, 0, 2, 0)
         tab_pass(wr, 0, 3, 0)
+        gather_words(1, 0)
+        first_tier(1, 0)
+        read_back(1, 0, 0)
+        read_back(1, 0, 1)
+        tab_pass(wq, 1, 0, 0)
+        tab_pass(wq, 1, 1, 0)
         first_tier(1, 1)
+        tab_pass(wq, 1, 2, 0)
+        tab_pass(wq, 1, 3, 0)
         leftover(1, 0, 0)
         read_back(1, 1, 0)
         leftover(1, 0, 1)
         read_back(1, 1, 1)
-        quantize_x(0, 0)
-        quantize_x(0, 1)
-        x_pass(0, 0)
-        x_pass(1, 0)
-        x_pass(2, 0)
-        x_pass(3, 0)
         second_tier(1, 0)
+        tab_pass(wr, 1, 0, 0)
+        tab_pass(wr, 1, 1, 0)
         leftover(1, 1, 0)
         tab_pass(wq, 0, 2, 1)
         tab_pass(wr, 0, 2, 1)
         leftover(1, 1, 1)
         tab_pass(wq, 0, 3, 1)
         tab_pass(wr, 0, 3, 1)
-        quantize_x(1, 0)
+        quantize_x(0, 0)
+        quantize_x(0, 1)
+        x_pass(0, 0)
+        x_pass(1, 0)
+        x_pass(2, 0)
+        x_pass(3, 0)
         second_tier(1, 1)
+        tab_pass(wr, 1, 2, 0)
+        tab_pass(wr, 1, 3, 0)
+        quantize_x(1, 0)
         quantize_x(1, 1)
         x_pass(0, 1)
         x_pass(1, 1)
         x_pass(2, 1)
         x_pass(3, 1)
-        gather_words(1, 0)
-        tab_pass(wq, 1, 0, 0)
-        tab_pass(wr, 1, 0, 0)
-        tab_pass(wq, 1, 1, 0)
-        tab_pass(wr, 1, 1, 0)
-        tab_pass(wq, 1, 2, 0)
-        tab_pass(wr, 1, 2, 0)
-        tab_pass(wq, 1, 3, 0)
-        tab_pass(wr, 1, 3, 0)
         gather_words(1, 1)
         tab_pass(wq, 1, 0, 1)
         tab_pass(wr, 1, 0, 1)

@@ -30,11 +30,11 @@ SHARE = {"words01": "w_raw00", "plane1": "w_bf00", "words10": "w_bf01", "words11
 
 
 def woven(ap):
-    return ap.rearrange("p (c i) t -> p c t i", i=4)
+    return ap.rearrange("p (c i) t -> p c t i", i=2)
 
 
 def by_rows(ap):
-    return ap.rearrange("p t (c i) -> p c t i", i=4)
+    return ap.rearrange("p t (c i) -> p c t i", i=2)
 
 
 def tile_list_tiert_none_kernel(tc, tab_words, tab_scales, wt, x, wx_words, wx_scales, offs, out):

@@ -24,9 +24,9 @@ JQ = 256
 NH = 256
 NC = 128
 LATE = ((2, 1), (3, 1),)
-ON_VECTOR = ((3, 1), )
-PLACED = {"eye": 0, "plane0": 0, "wq00_plane": 512, "wq01_plane": 768, "words00": 1024, "wq10_plane": 3072, "wq11_plane": 3328, "xq0_plane": 3584, "x_raw1": 4160, "res000": 4160, "res100": 6208, "res200": 8256, "res300": 10304}
-SHARE = {"words01": "w_raw00", "plane1": "w_bf00", "words10": "w_bf01", "words11": "x_bf11"}
+ON_VECTOR = ((1, 1), (3, 1), )
+PLACED = {"eye": 0, "plane0": 0, "wq00_plane": 512, "wq01_plane": 768, "words00": 1024, "wq10_plane": 3072, "wq11_plane": 3328, "xq0_plane": 3584, "x_raw10": 4160, "res000": 4160, "res100": 6208}
+SHARE = {"words01": "w_raw00", "plane1": "w_bf00"}
 
 
 def woven(ap):
@@ -156,7 +156,10 @@ def tile_list_tiert_none_kernel(tc, tab_words, tab_scales, wt, x, wx_words, wx_s
             codes, plane = xq[h]
             cols = slice(JQ * s, JQ * (s + 1))
             grouped = sb([P, JQ, PACK], BF16, f"x_bf{h}{s}")
-            nc.scalar.copy(out=woven(grouped[:]), in_=by_rows(x_raw[h, s][:]))
+            if (h, s) == (1, 1):
+                nc.vector.tensor_copy(out=woven(grouped[:]), in_=by_rows(x_raw[h, s][:]))
+            else:
+                nc.scalar.copy(out=woven(grouped[:]), in_=by_rows(x_raw[h, s][:]))
             nc.vector.quantize_mx(out=codes[:, cols].bitcast(FP8X4), scales=plane[:, cols], in_=grouped[:].rearrange("p w t -> p (w t)"))
 
         def add_pass(c, h, lhsT, lhsT_scale, rhs, rhs_scale):
@@ -197,15 +200,16 @@ def tile_list_tiert_none_kernel(tc, tab_words, tab_scales, wt, x, wx_words, wx_s
             load_ts(nc.sync, q)
         make_eye()
         nc.gpsimd.memset(wx_plane[:].bitcast(I32), 0)
+        for q in range(4):
+            load_ws(nc.gpsimd, q)
         load_tab(nc.sync, 0)
         load_w(nc.sync, 0, 1)
-        load_wxw(nc.sync)
-        load_tab(nc.sync, 1)
-        for q in range(4):
-            load_ws(nc.sync, q)
         load_w_pass(nc.sync, 1)
         load_x_half(nc.sync, 0)
-        load_x_half(nc.sync, 1)
+        load_tab(nc.sync, 1)
+        load_wxw(nc.sync)
+        load_x(nc.sync, 1, 0)
+        load_x(nc.sync, 1, 1)
         gather_plane(0)
         first_tier(0, 0)
         read_back(0, 0, 0)
@@ -221,62 +225,62 @@ def tile_list_tiert_none_kernel(tc, tab_words, tab_scales, wt, x, wx_words, wx_s
         read_back(0, 1, 1)
         tab_pass(wq, 0, 2, 0)
         tab_pass(wq, 0, 3, 0)
+        gather_words(0, 1)
+        tab_pass(wq, 0, 0, 1)
+        tab_pass(wq, 0, 1, 1)
         second_tier(0, 0)
         tab_pass(wr, 0, 0, 0)
         tab_pass(wr, 0, 1, 0)
-        gather_words(0, 1)
-        tab_pass(wq, 0, 0, 1)
         tab_pass(wr, 0, 0, 1)
-        tab_pass(wq, 0, 1, 1)
         tab_pass(wr, 0, 1, 1)
         leftover(0, 1, 0)
         leftover(0, 1, 1)
-        second_tier(0, 1)
-        tab_pass(wr, 0, 2, 0)
-        tab_pass(wr, 0, 3, 0)
-        gather_words(1, 0)
         first_tier(1, 0)
         read_back(1, 0, 0)
         read_back(1, 0, 1)
-        tab_pass(wq, 1, 0, 0)
-        tab_pass(wq, 1, 1, 0)
         first_tier(1, 1)
-        tab_pass(wq, 1, 2, 0)
-        tab_pass(wq, 1, 3, 0)
+        second_tier(0, 1)
+        tab_pass(wr, 0, 2, 0)
+        tab_pass(wr, 0, 3, 0)
         leftover(1, 0, 0)
         read_back(1, 1, 0)
         leftover(1, 0, 1)
         read_back(1, 1, 1)
+        quantize_x(0, 0)
         second_tier(1, 0)
-        tab_pass(wr, 1, 0, 0)
-        tab_pass(wr, 1, 1, 0)
         leftover(1, 1, 0)
         tab_pass(wq, 0, 2, 1)
         tab_pass(wr, 0, 2, 1)
         leftover(1, 1, 1)
         tab_pass(wq, 0, 3, 1)
         tab_pass(wr, 0, 3, 1)
-        quantize_x(0, 0)
         quantize_x(0, 1)
         x_pass(0, 0)
         x_pass(1, 0)
         x_pass(2, 0)
         x_pass(3, 0)
         second_tier(1, 1)
+        gather_words(1, 0)
+        tab_pass(wq, 1, 0, 0)
+        tab_pass(wr, 1, 0, 0)
+        tab_pass(wq, 1, 1, 0)
+        tab_pass(wr, 1, 1, 0)
+        tab_pass(wq, 1, 2, 0)
         tab_pass(wr, 1, 2, 0)
+        tab_pass(wq, 1, 3, 0)
         tab_pass(wr, 1, 3, 0)
-        quantize_x(1, 0)
-        quantize_x(1, 1)
-        x_pass(0, 1)
-        x_pass(1, 1)
-        x_pass(2, 1)
-        x_pass(3, 1)
         gather_words(1, 1)
         tab_pass(wq, 1, 0, 1)
         tab_pass(wr, 1, 0, 1)
         tab_pass(wq, 1, 1, 1)
         tab_pass(wr, 1, 1, 1)
+        quantize_x(1, 0)
+        quantize_x(1, 1)
+        x_pass(0, 1)
+        x_pass(1, 1)
+        x_pass(2, 1)
         tab_pass(wq, 1, 2, 1)
         tab_pass(wr, 1, 2, 1)
+        x_pass(3, 1)
         tab_pass(wq, 1, 3, 1)
         tab_pass(wr, 1, 3, 1)

@@ -15,18 +15,24 @@ U8 = mybir.dt.uint8
 FP8X4 = mybir.dt.float8_e4m3fn_x4
 FP4X4 = mybir.dt.float4_e2m1fn_x4
 SUB = mybir.AluOpType.subtract
+BYTES_OF = {F32: 4, BF16: 2, I32: 4, U32: 4, U8: 1}
 
 P = 128
 PACK = 4
 KP = P * PACK
-JH = 512
 JQ = 256
 NH = 256
 NC = 128
-LATE = ((2, 1), (3, 1),)
-ON_VECTOR = ((1, 1), (3, 1), )
-PLACED = {"eye": 0, "plane0": 0, "wq00_plane": 512, "wq01_plane": 768, "words00": 1024, "wq10_plane": 3072, "wq11_plane": 3328, "xq0_plane": 3584, "x_raw10": 4160, "res000": 4160, "res100": 6208}
-SHARE = {"words01": "w_raw00", "plane1": "w_bf00"}
+SPANS = ((0, 512), (512, 768), (768, 1024))
+LATE_BANKS = ("shared0", "shared1", "bank0", "bank1")
+MARGINS = {"x_raw2": 2048, "x_bf2": 2048}
+HOSTS = {
+    "plane0": ("eye", 0), "wq00_plane": ("eye", 512), "wq01_plane": ("eye", 768), "words00": ("eye", 1024),
+    "plane1": ("w_bf00", 0), "words01": ("w_raw00", 0), "words10": ("w_bf11", 0), "words11": ("r_bf01", 0),
+    "r_bf11": ("x_raw0", 0), "words02": ("x_raw1", 0), "wr11_plane": ("x_raw1", 1024), "x_bf3": ("tab_raw1", 0),
+    "res00": ("x_raw2", -1984), "res10": ("x_raw2", 64), "res20": ("x_raw2", 2112),
+    "res30": ("x_bf2", -1984), "words12": ("x_bf2", 64),
+}
 
 
 def woven(ap):
@@ -41,13 +47,22 @@ def tile_list_tiert_none_kernel(tc, tab_words, tab_scales, wt, x, wx_words, wx_s
     nc = tc.nc
     with ExitStack() as ctx:
         keep = ctx.enter_context(tc.tile_pool(name="keep", bufs=1))
-        reuse = ctx.enter_context(tc.tile_pool(name="reuse", bufs=1))
+        work = ctx.enter_context(tc.tile_pool(name="work", bufs=1))
         psum = ctx.enter_context(tc.psum_pool(name="psum", bufs=1))
+        where = {"end": 0}
 
         def sb(shape, dtype, name):
-            if name in PLACED:
-                return reuse.tile(shape, dtype, name=name, align_bytes=64, offset=PLACED[name])
-            return keep.tile(shape, dtype, name=name, tag=SHARE.get(name, name), align_bytes=64)
+            size = BYTES_OF[dtype]
+            for extent in shape[1:]:
+                size = size * extent
+            if name in HOSTS:
+                host, inside = HOSTS[name]
+                where[name] = where[host] + inside
+            else:
+                margin = MARGINS.get(name, 0)
+                where[name] = where["end"] + margin
+                where["end"] = where[name] + (size + 63) // 64 * 64 + margin
+            return work.tile(shape, dtype, name=name, align_bytes=64, offset=where[name])
 
         offsets = keep.tile([P, J // 16], U16, name="offsets")
         tab_plane = sb([P, T], U8, "tab_plane")
@@ -57,12 +72,9 @@ def tile_list_tiert_none_kernel(tc, tab_words, tab_scales, wt, x, wx_words, wx_s
         eye = sb([P, 4 * 513 + 12], BF16, "eye")
         eye_codes = sb([P, KP], U32, "eye_codes")
         eye_plane = sb([P, KP], U8, "eye_plane")
-        w_raw, tab_raw, x_raw = {}, {}, {}
+        w_raw, w_bf, tab_raw, x_raw, x_bf = {}, {}, {}, {}, {}
         planes, words, wq, wr, xq, acc, back, r_bf = {}, {}, {}, {}, {}, {}, {}, {}
         done = {}
-
-        def load_offs():
-            nc.sync.dma_start(offsets[:], offs)
 
         def load_ts(eng, q):
             eng.dma_start(tab_plane[32 * q : 32 * q + 8, :].bitcast(I32), tab_scales[:, 4 * q : 4 * q + 4, :].bitcast(I32))
@@ -84,19 +96,18 @@ def tile_list_tiert_none_kernel(tc, tab_words, tab_scales, wt, x, wx_words, wx_s
                 w_raw[a, u] = whole[:, :, NH * u : NH * (u + 1)]
 
         def load_x_half(eng, h):
-            half = sb([P, PACK, JH], F32, f"x_raw{h}")
-            eng.dma_start(half[:], x[:, JH * h : JH * (h + 1)].rearrange("(p j) w -> p j w", j=PACK))
+            half = sb([P, PACK, 2 * JQ], F32, f"x_half{h}")
+            eng.dma_start(half[:], x[:, 2 * JQ * h : 2 * JQ * (h + 1)].rearrange("(p j) w -> p j w", j=PACK))
             for s in range(2):
-                x_raw[h, s] = half[:, :, JQ * s : JQ * (s + 1)]
+                x_raw[2 * h + s] = half[:, :, JQ * s : JQ * (s + 1)]
 
         def load_tab(eng, a):
             tab_raw[a] = sb([P, T], I32, f"tab_raw{a}")
             eng.dma_start(tab_raw[a][:], tab_words[a].rearrange("p t i -> p (t i)").bitcast(I32))
 
-        def load_x(eng, h, s):
-            x_raw[h, s] = sb([P, PACK, JQ], F32, f"x_raw{h}{s}")
-            j0 = JH * h + JQ * s
-            eng.dma_start(x_raw[h, s][:], x[:, j0 : j0 + JQ].rearrange("(p j) w -> p j w", j=PACK))
+        def load_x(eng, s):
+            x_raw[s] = sb([P, PACK, JQ], F32, f"x_raw{s}")
+            eng.dma_start(x_raw[s][:], x[:, JQ * s : JQ * (s + 1)].rearrange("(p j) w -> p j w", j=PACK))
 
         def make_eye():
             make_identity(nc, ident[:])
@@ -108,12 +119,13 @@ def tile_list_tiert_none_kernel(tc, tab_words, tab_scales, wt, x, wx_words, wx_s
             nc.vector.quantize_mx(out=eye_codes[:].bitcast(FP8X4), scales=eye_plane[:], in_=eye[:, 0 : 4 * KP])
 
         def gather_plane(h):
-            planes[h] = sb([P, JH], U8, f"plane{h}")
+            planes[h] = sb([P, 512], U8, f"plane{h}")
             nc.vector.tensor_copy(planes[h][:], tab_plane[:].indirect(offsets[:, 32 * h : 32 * (h + 1)]))
 
-        def gather_words(a, h):
-            words[a, h] = sb([P, JH], U32, f"words{a}{h}")
-            nc.vector.tensor_copy(words[a, h][:], tab_raw[a][:].bitcast(U32).indirect(offsets[:, 32 * h : 32 * (h + 1)]))
+        def gather_words(a, g):
+            j0, j1 = SPANS[g]
+            words[a, g] = sb([P, j1 - j0], U32, f"words{a}{g}")
+            nc.vector.tensor_copy(words[a, g][:], tab_raw[a][:].bitcast(U32).indirect(offsets[:, j0 // 16 : j1 // 16]))
 
         def quantize(grouped, width, name):
             codes = sb([P, width], U32, name + "_codes")
@@ -121,18 +133,20 @@ def tile_list_tiert_none_kernel(tc, tab_words, tab_scales, wt, x, wx_words, wx_s
             nc.vector.quantize_mx(out=codes[:].bitcast(FP8X4), scales=plane[:], in_=grouped[:].rearrange("p w t -> p (w t)"))
             return codes, plane
 
-        def first_tier(a, u):
-            grouped = sb([P, NH, PACK], BF16, f"w_bf{a}{u}")
-            nc.scalar.copy(out=woven(grouped[:]), in_=by_rows(w_raw[a, u][:]))
-            wq[a, u] = quantize(grouped, NH, f"wq{a}{u}")
+        def cast_w(a, u):
+            w_bf[a, u] = sb([P, NH, PACK], BF16, f"w_bf{a}{u}")
+            nc.scalar.copy(out=woven(w_bf[a, u][:]), in_=by_rows(w_raw[a, u][:]))
 
-        def read_back(a, u, v):
-            codes, plane = wq[a, u]
-            cols = slice(NC * v, NC * (v + 1))
-            back[a, u, v] = psum.tile([P, PACK, NC], F32, name="back", tag="shared", bufs=2)
+        def first_tier(a, u):
+            wq[a, u] = quantize(w_bf[a, u], NH, f"wq{a}{u}")
+
+        def read_back(a, c):
+            codes, plane = wq[a, c // 2]
+            cols = slice(NC * (c % 2), NC * (c % 2 + 1))
+            back[a, c] = psum.tile([P, PACK, NC], F32, name="back", tag=f"shared{c % 2}")
             for t in range(PACK):
                 nc.tensor.matmul_mx(
-                    out=back[a, u, v][:, t, :],
+                    out=back[a, c][:, t, :],
                     lhsT=eye_codes[:, P * t : P * (t + 1)].bitcast(FP8X4),
                     lhsT_scale=eye_plane[:, P * t : P * (t + 1)],
                     rhs=codes[:, cols].bitcast(FP8X4),
@@ -141,146 +155,180 @@ def tile_list_tiert_none_kernel(tc, tab_words, tab_scales, wt, x, wx_words, wx_s
                     stop=True,
                 )
 
-        def leftover(a, u, v):
-            cols = slice(NC * v, NC * (v + 1))
+        def leftover(a, c):
+            u = c // 2
+            cols = slice(NC * (c % 2), NC * (c % 2 + 1))
             if (a, u) not in r_bf:
                 r_bf[a, u] = sb([P, NH, PACK], BF16, f"r_bf{a}{u}")
-            nc.vector.tensor_tensor(out=woven(r_bf[a, u][:, cols, :]), in0=by_rows(w_raw[a, u][:, :, cols]), in1=by_rows(back[a, u, v][:]), op=SUB)
+            nc.vector.tensor_tensor(out=woven(r_bf[a, u][:, cols, :]), in0=by_rows(w_raw[a, u][:, :, cols]), in1=by_rows(back[a, c][:]), op=SUB)
 
         def second_tier(a, u):
             wr[a, u] = quantize(r_bf[a, u], NH, f"wr{a}{u}")
 
-        def quantize_x(h, s):
-            if h not in xq:
-                xq[h] = (sb([P, JH], U32, f"xq{h}_codes"), sb([P, JH], U8, f"xq{h}_plane"))
-            codes, plane = xq[h]
-            cols = slice(JQ * s, JQ * (s + 1))
-            grouped = sb([P, JQ, PACK], BF16, f"x_bf{h}{s}")
-            if (h, s) == (1, 1):
-                nc.vector.tensor_copy(out=woven(grouped[:]), in_=by_rows(x_raw[h, s][:]))
+        def cast_x(s, eng="scalar"):
+            x_bf[s] = sb([P, JQ, PACK], BF16, f"x_bf{s}")
+            if eng == "vector":
+                nc.vector.tensor_copy(out=woven(x_bf[s][:]), in_=by_rows(x_raw[s][:]))
             else:
-                nc.scalar.copy(out=woven(grouped[:]), in_=by_rows(x_raw[h, s][:]))
-            nc.vector.quantize_mx(out=codes[:, cols].bitcast(FP8X4), scales=plane[:, cols], in_=grouped[:].rearrange("p w t -> p (w t)"))
+                nc.scalar.copy(out=woven(x_bf[s][:]), in_=by_rows(x_raw[s][:]))
 
-        def add_pass(c, h, lhsT, lhsT_scale, rhs, rhs_scale):
-            count = done.get((c, h), 0)
-            if count == 0:
-                if (c, h) in LATE:
-                    acc[c, h] = psum.tile([P, JH], F32, name="late", tag="shared", bufs=2)
-                else:
-                    acc[c, h] = psum.tile([P, JH], F32, name=f"acc{c}{h}")
-            nc.tensor.matmul_mx(out=acc[c, h][:], lhsT=lhsT, lhsT_scale=lhsT_scale, rhs=rhs, rhs_scale=rhs_scale, start=(count == 0), stop=(count == 4))
-            done[c, h] = count + 1
-            if count == 4:
-                pieces = 2 if (c, h) == (3, 1) else 1
-                width = JH // pieces
-                for piece in range(pieces):
-                    cols = slice(width * piece, width * (piece + 1))
-                    res = sb([P, width], F32, f"res{c}{h}{piece}")
-                    if (c, h) in ON_VECTOR:
-                        nc.vector.tensor_copy(out=res[:], in_=acc[c, h][:, cols])
-                    else:
-                        nc.scalar.copy(out=res[:], in_=acc[c, h][:, cols])
-                    j0 = JH * h + width * piece
-                    nc.sync.dma_start(out[NC * c : NC * (c + 1), j0 : j0 + width], res[:])
+        def quantize_x(s):
+            g = max(s - 1, 0)
+            j0, j1 = SPANS[g]
+            if g not in xq:
+                xq[g] = (sb([P, j1 - j0], U32, f"xq{g}_codes"), sb([P, j1 - j0], U8, f"xq{g}_plane"))
+            codes, plane = xq[g]
+            cols = slice(JQ * s - j0, JQ * (s + 1) - j0)
+            nc.vector.quantize_mx(out=codes[:, cols].bitcast(FP8X4), scales=plane[:, cols], in_=x_bf[s][:].rearrange("p w t -> p (w t)"))
 
-        def tab_pass(tier, a, c, h):
+        def bank(c, g):
+            if g == 0:
+                key, tag, shape, first, count = (c, 0), f"bank{c}", [P, 512], 0, 5
+            elif g == 1:
+                key, tag, shape, first, count = (c // 2, 1), f"bank{4 + c // 2}", [P, 512], JQ * (c % 2), 12
+            else:
+                key, tag, shape, first, count = (c, 2), LATE_BANKS[c], [P, 512], 0, 6
+            if key not in acc:
+                acc[key] = psum.tile(shape, F32, name=f"acc{key[0]}{key[1]}", tag=tag)
+                done[key] = 0
+            return key, first, count
+
+        def add_pass(c, g, j0, j1, lhsT, lhsT_scale, rhs, rhs_scale):
+            key, first, count = bank(c, g)
+            nc.tensor.matmul_mx(
+                out=acc[key][:, first + j0 : first + j1], lhsT=lhsT, lhsT_scale=lhsT_scale, rhs=rhs, rhs_scale=rhs_scale,
+                start=(done[key] == 0), stop=(done[key] == count - 1),
+            )
+            done[key] = done[key] + 1
+
+        def tab_pass(tier, a, c, g):
             codes, plane = tier[a, c // 2]
             cols = slice(NC * (c % 2), NC * (c % 2 + 1))
-            add_pass(c, h, codes[:, cols].bitcast(FP8X4), plane[:, cols], words[a, h][:].bitcast(FP8X4), planes[h][4 * a : P, :])
+            j0, j1 = SPANS[g]
+            scale = planes[j0 // 512][4 * a : P, j0 % 512 : j0 % 512 + j1 - j0]
+            add_pass(c, g, 0, j1 - j0, codes[:, cols].bitcast(FP8X4), plane[:, cols], words[a, g][:].bitcast(FP8X4), scale)
 
-        def x_pass(c, h):
-            codes, plane = xq[h]
-            add_pass(c, h, wx_codes[:, 2 * NC * c : 2 * NC * (c + 1)].bitcast(FP4X4), wx_plane[:, NC * c : NC * (c + 1)], codes[:].bitcast(FP8X4), plane[:])
+        def x_pass(c, g):
+            codes, plane = xq[g]
+            j0, j1 = SPANS[g]
+            step = 512 if g == 0 else 128
+            for k in range(0, j1 - j0, step):
+                add_pass(c, g, k, k + step, wx_codes[:, 2 * NC * c : 2 * NC * (c + 1)].bitcast(FP4X4), wx_plane[:, NC * c : NC * (c + 1)],
+                         codes[:, k : k + step].bitcast(FP8X4), plane[:, k : k + step])
+
+        def store(i, g, eng, queue):
+            j0, j1 = SPANS[g]
+            width = 256 if g == 2 else 512
+            res = sb([P, width], F32, f"res{i}{g}")
+            if eng == "vector":
+                nc.vector.tensor_copy(out=res[:], in_=acc[i, g][:, 0:width])
+            else:
+                nc.scalar.copy(out=res[:], in_=acc[i, g][:, 0:width])
+            if g == 1:
+                queue.dma_start(out[NH * i : NH * (i + 1), j0:j1].rearrange("(c p) j -> p c j", p=P), res[:].rearrange("p (c j) -> p c j", c=2))
+            else:
+                queue.dma_start(out[NC * i : NC * (i + 1), j0:j1], res[:])
 
         nc.gpsimd.memset(tab_plane[:].bitcast(I32), 0)
-        load_offs()
+        nc.sync.dma_start(offsets[:], offs)
         load_w(nc.sync, 0, 0)
         for q in range(4):
             load_ts(nc.sync, q)
         make_eye()
         nc.gpsimd.memset(wx_plane[:].bitcast(I32), 0)
-        for q in range(4):
-            load_ws(nc.gpsimd, q)
         load_tab(nc.sync, 0)
         load_w(nc.sync, 0, 1)
-        load_w_pass(nc.sync, 1)
-        load_x_half(nc.sync, 0)
+        load_w(nc.sync, 1, 0)
+        load_w(nc.sync, 1, 1)
         load_tab(nc.sync, 1)
+        load_x(nc.sync, 0)
+        for q in range(4):
+            load_ws(nc.sync, q)
         load_wxw(nc.sync)
-        load_x(nc.sync, 1, 0)
-        load_x(nc.sync, 1, 1)
+        load_x(nc.sync, 1)
+        load_x(nc.sync, 2)
+        load_x(nc.sync, 3)
+        for a in range(2):
+            for u in range(2):
+                cast_w(a, u)
+        for s in range(3):
+            cast_x(s)
         gather_plane(0)
         first_tier(0, 0)
-        read_back(0, 0, 0)
-        read_back(0, 0, 1)
+        read_back(0, 0)
+        read_back(0, 1)
         gather_plane(1)
         gather_words(0, 0)
-        tab_pass(wq, 0, 0, 0)
-        tab_pass(wq, 0, 1, 0)
-        leftover(0, 0, 0)
-        leftover(0, 0, 1)
+        for c in (0, 1):
+            tab_pass(wq, 0, c, 0)
+        leftover(0, 0)
+        leftover(0, 1)
         first_tier(0, 1)
-        read_back(0, 1, 0)
-        read_back(0, 1, 1)
-        tab_pass(wq, 0, 2, 0)
-        tab_pass(wq, 0, 3, 0)
+        read_back(0, 2)
+        read_back(0, 3)
+        for c in (2, 3):
+            tab_pass(wq, 0, c, 0)
         gather_words(0, 1)
-        tab_pass(wq, 0, 0, 1)
-        tab_pass(wq, 0, 1, 1)
         second_tier(0, 0)
-        tab_pass(wr, 0, 0, 0)
-        tab_pass(wr, 0, 1, 0)
-        tab_pass(wr, 0, 0, 1)
-        tab_pass(wr, 0, 1, 1)
-        leftover(0, 1, 0)
-        leftover(0, 1, 1)
+        for c in (0, 1):
+            tab_pass(wr, 0, c, 0)
+        for c in (0, 1):
+            tab_pass(wq, 0, c, 1)
+            tab_pass(wr, 0, c, 1)
+        leftover(0, 2)
+        leftover(0, 3)
+        for c in (2, 3):
+            tab_pass(wq, 0, c, 1)
         first_tier(1, 0)
-        read_back(1, 0, 0)
-        read_back(1, 0, 1)
+        read_back(1, 0)
+        read_back(1, 1)
         first_tier(1, 1)
         second_tier(0, 1)
-        tab_pass(wr, 0, 2, 0)
-        tab_pass(wr, 0, 3, 0)
-        leftover(1, 0, 0)
-        read_back(1, 1, 0)
-        leftover(1, 0, 1)
-        read_back(1, 1, 1)
-        quantize_x(0, 0)
-        second_tier(1, 0)
-        leftover(1, 1, 0)
-        tab_pass(wq, 0, 2, 1)
-        tab_pass(wr, 0, 2, 1)
-        leftover(1, 1, 1)
-        tab_pass(wq, 0, 3, 1)
-        tab_pass(wr, 0, 3, 1)
-        quantize_x(0, 1)
-        x_pass(0, 0)
-        x_pass(1, 0)
-        x_pass(2, 0)
-        x_pass(3, 0)
-        second_tier(1, 1)
+        for g in (0, 1):
+            for c in (2, 3):
+                tab_pass(wr, 0, c, g)
         gather_words(1, 0)
-        tab_pass(wq, 1, 0, 0)
-        tab_pass(wr, 1, 0, 0)
-        tab_pass(wq, 1, 1, 0)
-        tab_pass(wr, 1, 1, 0)
-        tab_pass(wq, 1, 2, 0)
-        tab_pass(wr, 1, 2, 0)
+        for c in range(3):
+            tab_pass(wq, 1, c, 0)
+        leftover(1, 0)
+        read_back(1, 2)
         tab_pass(wq, 1, 3, 0)
-        tab_pass(wr, 1, 3, 0)
+        leftover(1, 1)
+        read_back(1, 3)
         gather_words(1, 1)
-        tab_pass(wq, 1, 0, 1)
-        tab_pass(wr, 1, 0, 1)
-        tab_pass(wq, 1, 1, 1)
-        tab_pass(wr, 1, 1, 1)
-        quantize_x(1, 0)
-        quantize_x(1, 1)
-        x_pass(0, 1)
-        x_pass(1, 1)
-        x_pass(2, 1)
-        tab_pass(wq, 1, 2, 1)
-        tab_pass(wr, 1, 2, 1)
-        x_pass(3, 1)
-        tab_pass(wq, 1, 3, 1)
-        tab_pass(wr, 1, 3, 1)
+        for c in range(4):
+            tab_pass(wq, 1, c, 1)
+        second_tier(1, 0)
+        for g in (0, 1):
+            for c in (0, 1):
+                tab_pass(wr, 1, c, g)
+        quantize_x(0)
+        leftover(1, 2)
+        leftover(1, 3)
+        quantize_x(1)
+        for c in range(4):
+            x_pass(c, 0)
+        store(0, 0, "scalar", nc.sync)
+        store(1, 0, "scalar", nc.sync)
+        second_tier(1, 1)
+        for c in (2, 3):
+            tab_pass(wr, 1, c, 0)
+            store(c, 0, "scalar", nc.sync)
+        gather_words(0, 2)
+        quantize_x(2)
+        for c in (0, 1):
+            x_pass(c, 1)
+        store(0, 1, "scalar", nc.sync)
+        for c in (2, 3):
+            tab_pass(wr, 1, c, 1)
+            x_pass(c, 1)
+        store(1, 1, "scalar", nc.sync)
+        gather_words(1, 2)
+        cast_x(3, "vector")
+        quantize_x(3)
+        for c in range(4):
+            for a in range(2):
+                tab_pass(wq, a, c, 2)
+                tab_pass(wr, a, c, 2)
+            x_pass(c, 2)
+            store(c, 2, "scalar", nc.sync)

@@ -25,13 +25,13 @@ NH = 256
 NC = 128
 SPANS = ((0, 512), (512, 768), (768, 1024))
 LATE_BANKS = ("shared0", "shared1", "bank0", "bank1")
-MARGINS = {"x_raw2": 2048, "x_bf2": 2048}
+MARGINS = {"x_raw2": 2048}
 HOSTS = {
-    "plane0": ("eye", 0), "wq00_plane": ("eye", 512), "wq01_plane": ("eye", 768), "words00": ("eye", 1024),
-    "plane1": ("w_bf00", 0), "words01": ("w_raw00", 0), "words10": ("w_bf11", 0), "words11": ("r_bf01", 0),
-    "r_bf11": ("x_raw0", 0), "words02": ("x_raw1", 0), "wr11_plane": ("x_raw1", 1024), "x_bf3": ("tab_raw1", 0),
-    "res00": ("x_raw2", -1984), "res10": ("x_raw2", 64), "res20": ("x_raw2", 2112),
-    "res30": ("x_bf2", -1984), "words12": ("x_bf2", 64),
+    "plane": ("eye", 0), "wq00_plane": ("eye", 1024), "wq01_plane": ("eye", 1280), "words00": ("eye", 1536),
+    "words01": ("w_raw00", 0), "words10": ("w_bf11", 0), "words11": ("r_bf01", 0),
+    "r_chunk12": ("x_raw0", 0), "r_chunk13": ("x_raw1", 0), "words02": ("x_raw1", 1024),
+    "res00": ("x_raw2", -1984), "words12": ("x_raw2", 64), "res10": ("x_raw2", 1088), "res20": ("x_raw2", 3136),
+    "res30": ("x_bf2", 0),
 }
 
 
@@ -118,9 +118,9 @@ def tile_list_tiert_none_kernel(tc, tab_words, tab_scales, wt, x, wx_words, wx_s
             )
             nc.vector.quantize_mx(out=eye_codes[:].bitcast(FP8X4), scales=eye_plane[:], in_=eye[:, 0 : 4 * KP])
 
-        def gather_plane(h):
-            planes[h] = sb([P, 512], U8, f"plane{h}")
-            nc.vector.tensor_copy(planes[h][:], tab_plane[:].indirect(offsets[:, 32 * h : 32 * (h + 1)]))
+        def gather_plane():
+            planes[0] = sb([P, J], U8, "plane")
+            nc.vector.tensor_copy(planes[0][:], tab_plane[:].indirect(offsets[:]))
 
         def gather_words(a, g):
             j0, j1 = SPANS[g]
@@ -165,6 +165,14 @@ def tile_list_tiert_none_kernel(tc, tab_words, tab_scales, wt, x, wx_words, wx_s
         def second_tier(a, u):
             wr[a, u] = quantize(r_bf[a, u], NH, f"wr{a}{u}")
 
+        def leftover_chunk(a, c):
+            cols = slice(NC * (c % 2), NC * (c % 2 + 1))
+            r_bf[a, "chunk", c] = sb([P, NC, PACK], BF16, f"r_chunk{a}{c}")
+            nc.vector.tensor_tensor(out=woven(r_bf[a, "chunk", c][:]), in0=by_rows(w_raw[a, c // 2][:, :, cols]), in1=by_rows(back[a, c][:]), op=SUB)
+
+        def second_tier_chunk(a, c):
+            wr[a, "chunk", c] = quantize(r_bf[a, "chunk", c], NC, f"wr_chunk{a}{c}")
+
         def cast_x(s, eng="scalar"):
             x_bf[s] = sb([P, JQ, PACK], BF16, f"x_bf{s}")
             if eng == "vector":
@@ -202,10 +210,14 @@ def tile_list_tiert_none_kernel(tc, tab_words, tab_scales, wt, x, wx_words, wx_s
             done[key] = done[key] + 1
 
         def tab_pass(tier, a, c, g):
-            codes, plane = tier[a, c // 2]
-            cols = slice(NC * (c % 2), NC * (c % 2 + 1))
+            if (a, "chunk", c) in tier:
+                codes, plane = tier[a, "chunk", c]
+                cols = slice(0, NC)
+            else:
+                codes, plane = tier[a, c // 2]
+                cols = slice(NC * (c % 2), NC * (c % 2 + 1))
             j0, j1 = SPANS[g]
-            scale = planes[j0 // 512][4 * a : P, j0 % 512 : j0 % 512 + j1 - j0]
+            scale = planes[0][4 * a : P, j0:j1]
             add_pass(c, g, 0, j1 - j0, codes[:, cols].bitcast(FP8X4), plane[:, cols], words[a, g][:].bitcast(FP8X4), scale)
 
         def x_pass(c, g):
@@ -230,8 +242,8 @@ def tile_list_tiert_none_kernel(tc, tab_words, tab_scales, wt, x, wx_words, wx_s
                 queue.dma_start(out[NC * i : NC * (i + 1), j0:j1], res[:])
 
         nc.gpsimd.memset(tab_plane[:].bitcast(I32), 0)
-        nc.sync.dma_start(offsets[:], offs)
         load_w(nc.sync, 0, 0)
+        nc.sync.dma_start(offsets[:], offs)
         for q in range(4):
             load_ts(nc.sync, q)
         make_eye()
@@ -253,11 +265,10 @@ def tile_list_tiert_none_kernel(tc, tab_words, tab_scales, wt, x, wx_words, wx_s
                 cast_w(a, u)
         for s in range(3):
             cast_x(s)
-        gather_plane(0)
+        gather_plane()
         first_tier(0, 0)
         read_back(0, 0)
         read_back(0, 1)
-        gather_plane(1)
         gather_words(0, 0)
         for c in (0, 1):
             tab_pass(wq, 0, c, 0)
@@ -303,32 +314,38 @@ def tile_list_tiert_none_kernel(tc, tab_words, tab_scales, wt, x, wx_words, wx_s
             for c in (0, 1):
                 tab_pass(wr, 1, c, g)
         quantize_x(0)
-        leftover(1, 2)
-        leftover(1, 3)
+        leftover_chunk(1, 2)
         quantize_x(1)
         for c in range(4):
             x_pass(c, 0)
         store(0, 0, "scalar", nc.sync)
         store(1, 0, "scalar", nc.sync)
-        second_tier(1, 1)
-        for c in (2, 3):
-            tab_pass(wr, 1, c, 0)
-            store(c, 0, "scalar", nc.sync)
+        second_tier_chunk(1, 2)
+        leftover_chunk(1, 3)
+        tab_pass(wr, 1, 2, 0)
+        store(2, 0, "scalar", nc.sync)
+        tab_pass(wr, 1, 2, 1)
         gather_words(0, 2)
+        second_tier_chunk(1, 3)
+        for c in (0, 1):
+            tab_pass(wq, 0, c, 2)
+            tab_pass(wr, 0, c, 2)
+        tab_pass(wr, 1, 3, 0)
+        store(3, 0, "scalar", nc.sync)
         quantize_x(2)
         for c in (0, 1):
             x_pass(c, 1)
         store(0, 1, "scalar", nc.sync)
+        tab_pass(wr, 1, 3, 1)
         for c in (2, 3):
-            tab_pass(wr, 1, c, 1)
             x_pass(c, 1)
         store(1, 1, "scalar", nc.sync)
-        gather_words(1, 2)
         cast_x(3, "vector")
+        gather_words(1, 2)
         quantize_x(3)
         for c in range(4):
-            for a in range(2):
-                tab_pass(wq, a, c, 2)
-                tab_pass(wr, a, c, 2)
+            for a in range(2 if c > 1 else 1, 0, -1):
+                tab_pass(wq, 2 - a if c > 1 else 1, c, 2)
+                tab_pass(wr, 2 - a if c > 1 else 1, c, 2)
             x_pass(c, 2)
             store(c, 2, "scalar", nc.sync)

@@ -1,7 +1,6 @@
 from contextlib import ExitStack
 
 import concourse.mybir as mybir
-from concourse.masks import make_identity
 
 K, L, N, T, J = 1024, 512, 512, 2048, 1024
 FLOPS = 3221225472
@@ -25,13 +24,13 @@ NH = 256
 NC = 128
 SPANS = ((0, 512), (512, 768), (768, 1024))
 LATE_BANKS = ("shared0", "shared1", "bank0", "bank1")
-MARGINS = {"x_raw2": 2048}
+MARGINS = {"x_raw2": 2048, "x_raw3": 2048}
 HOSTS = {
     "plane": ("eye", 0), "wq00_plane": ("eye", 1024), "wq01_plane": ("eye", 1280), "words00": ("eye", 1536),
-    "words01": ("w_raw00", 0), "words10": ("w_bf11", 0), "words11": ("r_bf01", 0),
-    "r_chunk12": ("x_raw0", 0), "r_chunk13": ("x_raw1", 0), "words02": ("x_raw1", 1024),
-    "res00": ("x_raw2", -1984), "words12": ("x_raw2", 64), "res10": ("x_raw2", 1088), "res20": ("x_raw2", 3136),
-    "res30": ("x_bf2", 0),
+    "words01": ("w_raw00", 0), "words10": ("w_bf11", 0),
+    "r_chunk12": ("x_raw1", 0), "words11": ("x_raw1", 1024), "r_chunk13": ("x_raw1", 2048), "words02": ("x_raw1", 3072),
+    "res00": ("x_raw2", -1984), "words12": ("x_raw2", 64), "res10": ("x_raw2", 1088),
+    "res20": ("x_raw3", -1984), "res30": ("x_raw3", 64), "res01": ("x_raw3", 2112), "res11": ("x_bf3", 0),
 }
 
 
@@ -68,8 +67,8 @@ def tile_list_tiert_none_kernel(tc, tab_words, tab_scales, wt, x, wx_words, wx_s
         tab_plane = sb([P, T], U8, "tab_plane")
         wx_plane = sb([P, N], U8, "wx_plane")
         wx_codes = sb([P, 2 * N], U8, "wx_codes")
-        ident = sb([P, P], BF16, "ident")
-        eye = sb([P, 4 * 513 + 12], BF16, "eye")
+        ramp = sb([P, KP], BF16, "ramp")
+        eye = sb([P, PACK * KP], BF16, "eye")
         eye_codes = sb([P, KP], U32, "eye_codes")
         eye_plane = sb([P, KP], U8, "eye_plane")
         w_raw, w_bf, tab_raw, x_raw, x_bf = {}, {}, {}, {}, {}
@@ -110,17 +109,17 @@ def tile_list_tiert_none_kernel(tc, tab_words, tab_scales, wt, x, wx_words, wx_s
             eng.dma_start(x_raw[s][:], x[:, JQ * s : JQ * (s + 1)].rearrange("(p j) w -> p j w", j=PACK))
 
         def make_eye():
-            make_identity(nc, ident[:])
-            nc.vector.memset(eye[:].bitcast(I32), 0)
-            nc.vector.tensor_copy(
-                out=eye[:, 0 : 4 * 513].rearrange("p (j m) -> p j m", j=4)[:, :, 0:512:4],
-                in_=ident[:].unsqueeze(1).to_broadcast([P, 4, P]),
-            )
+            nc.gpsimd.iota(ramp[:], pattern=[[1, KP]], base=0, channel_multiplier=-PACK, allow_small_or_imprecise_dtypes=True)
+            for t in range(PACK):
+                nc.vector.tensor_scalar(out=eye[:, KP * t : KP * (t + 1)], in0=ramp[:], scalar1=float(t), scalar2=None, op0=mybir.AluOpType.is_equal)
+
+        def quantize_eye():
             nc.vector.quantize_mx(out=eye_codes[:].bitcast(FP8X4), scales=eye_plane[:], in_=eye[:, 0 : 4 * KP])
 
         def gather_plane():
             planes[0] = sb([P, J], U8, "plane")
             nc.vector.tensor_copy(planes[0][:], tab_plane[:].indirect(offsets[:]))
+
 
         def gather_words(a, g):
             j0, j1 = SPANS[g]
@@ -241,13 +240,14 @@ def tile_list_tiert_none_kernel(tc, tab_words, tab_scales, wt, x, wx_words, wx_s
             else:
                 queue.dma_start(out[NC * i : NC * (i + 1), j0:j1], res[:])
 
-        nc.gpsimd.memset(tab_plane[:].bitcast(I32), 0)
+        nc.vector.memset(tab_plane[:].bitcast(I32), 0)
         load_w(nc.sync, 0, 0)
         nc.sync.dma_start(offsets[:], offs)
         for q in range(4):
             load_ts(nc.sync, q)
+        nc.vector.memset(wx_plane[:].bitcast(I32), 0)
         make_eye()
-        nc.gpsimd.memset(wx_plane[:].bitcast(I32), 0)
+        quantize_eye()
         load_tab(nc.sync, 0)
         load_w(nc.sync, 0, 1)
         load_w(nc.sync, 1, 0)
@@ -263,7 +263,7 @@ def tile_list_tiert_none_kernel(tc, tab_words, tab_scales, wt, x, wx_words, wx_s
         for a in range(2):
             for u in range(2):
                 cast_w(a, u)
-        for s in range(3):
+        for s in range(4):
             cast_x(s)
         gather_plane()
         first_tier(0, 0)
@@ -306,21 +306,23 @@ def tile_list_tiert_none_kernel(tc, tab_words, tab_scales, wt, x, wx_words, wx_s
         tab_pass(wq, 1, 3, 0)
         leftover(1, 1)
         read_back(1, 3)
-        gather_words(1, 1)
-        for c in range(4):
-            tab_pass(wq, 1, c, 1)
-        second_tier(1, 0)
-        for g in (0, 1):
-            for c in (0, 1):
-                tab_pass(wr, 1, c, g)
         quantize_x(0)
-        leftover_chunk(1, 2)
+        second_tier(1, 0)
+        for c in (0, 1):
+            tab_pass(wr, 1, c, 0)
         quantize_x(1)
         for c in range(4):
             x_pass(c, 0)
         store(0, 0, "scalar", nc.sync)
         store(1, 0, "scalar", nc.sync)
+        leftover_chunk(1, 2)
+        gather_words(1, 1)
+        for c in (0, 1):
+            tab_pass(wq, 1, c, 1)
+            tab_pass(wr, 1, c, 1)
         second_tier_chunk(1, 2)
+        for c in (2, 3):
+            tab_pass(wq, 1, c, 1)
         leftover_chunk(1, 3)
         tab_pass(wr, 1, 2, 0)
         store(2, 0, "scalar", nc.sync)
@@ -340,7 +342,6 @@ def tile_list_tiert_none_kernel(tc, tab_words, tab_scales, wt, x, wx_words, wx_s
         for c in (2, 3):
             x_pass(c, 1)
         store(1, 1, "scalar", nc.sync)
-        cast_x(3, "vector")
         gather_words(1, 2)
         quantize_x(3)
         for c in range(4):

@@ -24,13 +24,13 @@ NH = 256
 NC = 128
 SPANS = ((0, 512), (512, 768), (768, 1024))
 LATE_BANKS = ("shared0", "shared1", "bank0", "bank1")
-MARGINS = {"x_raw2": 2048, "x_raw3": 2048}
+MARGINS = {"x_raw2": 2048, "x_raw3": 2048, "x_bf3": 2048}
 HOSTS = {
     "plane": ("eye", 0), "wq00_plane": ("eye", 1024), "wq01_plane": ("eye", 1280), "words00": ("eye", 1536),
     "words01": ("w_raw00", 0), "words10": ("w_bf11", 0),
     "r_chunk12": ("x_raw1", 0), "words11": ("x_raw1", 1024), "r_chunk13": ("x_raw1", 2048), "words02": ("x_raw1", 3072),
     "res00": ("x_raw2", -1984), "words12": ("x_raw2", 64), "res10": ("x_raw2", 1088),
-    "res20": ("x_raw3", -1984), "res30": ("x_raw3", 64), "res01": ("x_raw3", 2112), "res11": ("x_bf3", 0),
+    "res20": ("x_raw3", -1984), "res30": ("x_raw3", 64), "res01": ("x_bf3", -1984), "res11": ("x_bf3", 64),
 }
 
 
@@ -67,7 +67,7 @@ def tile_list_tiert_none_kernel(tc, tab_words, tab_scales, wt, x, wx_words, wx_s
         tab_plane = sb([P, T], U8, "tab_plane")
         wx_plane = sb([P, N], U8, "wx_plane")
         wx_codes = sb([P, 2 * N], U8, "wx_codes")
-        ramp = sb([P, KP], BF16, "ramp")
+        ramp = sb([P, KP // 2], BF16, "ramp")
         eye = sb([P, PACK * KP], BF16, "eye")
         eye_codes = sb([P, KP], U32, "eye_codes")
         eye_plane = sb([P, KP], U8, "eye_plane")
@@ -109,9 +109,11 @@ def tile_list_tiert_none_kernel(tc, tab_words, tab_scales, wt, x, wx_words, wx_s
             eng.dma_start(x_raw[s][:], x[:, JQ * s : JQ * (s + 1)].rearrange("(p j) w -> p j w", j=PACK))
 
         def make_eye():
-            nc.gpsimd.iota(ramp[:], pattern=[[1, KP]], base=0, channel_multiplier=-PACK, allow_small_or_imprecise_dtypes=True)
+            nc.gpsimd.iota(ramp[:], pattern=[[1, KP // 2]], base=P, channel_multiplier=-PACK, allow_small_or_imprecise_dtypes=True)
             for t in range(PACK):
-                nc.vector.tensor_scalar(out=eye[:, KP * t : KP * (t + 1)], in0=ramp[:], scalar1=float(t), scalar2=None, op0=mybir.AluOpType.is_equal)
+                for h in range(2):
+                    first = KP * t + KP // 2 * h
+                    nc.vector.tensor_scalar(out=eye[:, first : first + KP // 2], in0=ramp[:], scalar1=float(P + t - KP // 2 * h), scalar2=None, op0=mybir.AluOpType.is_equal)
 
         def quantize_eye():
             nc.vector.quantize_mx(out=eye_codes[:].bitcast(FP8X4), scales=eye_plane[:], in_=eye[:, 0 : 4 * KP])
@@ -337,13 +339,13 @@ def tile_list_tiert_none_kernel(tc, tab_words, tab_scales, wt, x, wx_words, wx_s
         quantize_x(2)
         for c in (0, 1):
             x_pass(c, 1)
-        store(0, 1, "scalar", nc.sync)
         tab_pass(wr, 1, 3, 1)
         for c in (2, 3):
             x_pass(c, 1)
-        store(1, 1, "scalar", nc.sync)
         gather_words(1, 2)
         quantize_x(3)
+        store(0, 1, "vector", nc.sync)
+        store(1, 1, "vector", nc.sync)
         for c in range(4):
             for a in range(2 if c > 1 else 1, 0, -1):
                 tab_pass(wq, 2 - a if c > 1 else 1, c, 2)

@@ -24,13 +24,12 @@ NH = 256
 NC = 128
 SPANS = ((0, 512), (512, 768), (768, 1024))
 LATE_BANKS = ("shared0", "shared1", "bank0", "bank1")
-MARGINS = {"x_raw2": 2048, "x_raw3": 2048, "x_bf3": 2048}
+MARGINS = {}
 HOSTS = {
-    "plane": ("eye", 0), "wq00_plane": ("eye", 1024), "wq01_plane": ("eye", 1280), "words00": ("eye", 1536),
-    "words01": ("w_raw00", 0), "words10": ("w_bf11", 0),
-    "r_chunk12": ("x_raw1", 0), "words11": ("x_raw1", 1024), "r_chunk13": ("x_raw1", 2048), "words02": ("x_raw1", 3072),
-    "res00": ("x_raw2", -1984), "words12": ("x_raw2", 64), "res10": ("x_raw2", 1088),
-    "res20": ("x_raw3", -1984), "res30": ("x_raw3", 64), "res01": ("x_bf3", -1984), "res11": ("x_bf3", 64),
+    "plane_early": ("eye", 0), "wq00_codes": ("eye", 1024),
+    "wq01_codes": ("w_raw00", 0), "words00": ("w_raw00", 1024), "words01": ("w_raw00", 3072),
+    "words10": ("w_bf11", 0), "words11": ("w_raw10", 0), "r_bf11": ("x_raw1", 0),
+    "wr11_codes": ("x_raw3", 0), "plane_late": ("x_raw3", 1024), "words02": ("x_raw3", 2048), "words12": ("x_raw3", 3072),
 }
 
 
@@ -73,7 +72,7 @@ def tile_list_tiert_none_kernel(tc, tab_words, tab_scales, wt, x, wx_words, wx_s
         eye_plane = sb([P, KP], U8, "eye_plane")
         w_raw, w_bf, tab_raw, x_raw, x_bf = {}, {}, {}, {}, {}
         planes, words, wq, wr, xq, acc, back, r_bf = {}, {}, {}, {}, {}, {}, {}, {}
-        done = {}
+        done, parked, results = {}, {}, {}
 
         def load_ts(eng, q):
             eng.dma_start(tab_plane[32 * q : 32 * q + 8, :].bitcast(I32), tab_scales[:, 4 * q : 4 * q + 4, :].bitcast(I32))
@@ -118,9 +117,9 @@ def tile_list_tiert_none_kernel(tc, tab_words, tab_scales, wt, x, wx_words, wx_s
         def quantize_eye():
             nc.vector.quantize_mx(out=eye_codes[:].bitcast(FP8X4), scales=eye_plane[:], in_=eye[:, 0 : 4 * KP])
 
-        def gather_plane():
-            planes[0] = sb([P, J], U8, "plane")
-            nc.vector.tensor_copy(planes[0][:], tab_plane[:].indirect(offsets[:]))
+        def gather_plane(h):
+            planes[h] = sb([P, J // 2], U8, f"plane{h}")
+            nc.vector.tensor_copy(planes[h][:], tab_plane[:].indirect(offsets[:, 32 * h : 32 * (h + 1)]))
 
 
         def gather_words(a, g):
@@ -162,6 +161,36 @@ def tile_list_tiert_none_kernel(tc, tab_words, tab_scales, wt, x, wx_words, wx_s
             if (a, u) not in r_bf:
                 r_bf[a, u] = sb([P, NH, PACK], BF16, f"r_bf{a}{u}")
             nc.vector.tensor_tensor(out=woven(r_bf[a, u][:, cols, :]), in0=by_rows(w_raw[a, u][:, :, cols]), in1=by_rows(back[a, c][:]), op=SUB)
+
+        def park(a, c):
+            parked[a, c] = sb([P, NC, PACK], F32, f"parked{a}{c}")
+            nc.scalar.copy(out=parked[a, c][:], in_=back[a, c][:].rearrange("p t n -> p n t"))
+
+        def leftover_pool(a, c):
+            u = c // 2
+            cols = slice(NC * (c % 2), NC * (c % 2 + 1))
+            if (a, u) not in r_bf:
+                r_bf[a, u] = sb([P, NH, PACK], BF16, f"r_bf{a}{u}")
+            nc.gpsimd.tensor_tensor(out=r_bf[a, u][:, cols, :], in0=w_raw[a, u][:, :, cols].rearrange("p t n -> p n t"), in1=parked[a, c][:], op=SUB)
+
+        def gather_planes():
+            whole = sb([P, J], U8, "plane")
+            nc.vector.tensor_copy(whole[:], tab_plane[:].indirect(offsets[:]))
+            planes[0], planes[1] = whole[:, 0:512], whole[:, 512:J]
+
+        def warm_up(count):
+            spare = psum.tile([P, KP], F32, name="spare", tag="bank3")
+            codes, plane = wq[0, 0]
+            for i in range(count):
+                nc.tensor.matmul_mx(out=spare[:], lhsT=codes[:, 0:NC].bitcast(FP8X4), lhsT_scale=plane[:, 0:NC],
+                                    rhs=eye_codes[:].bitcast(FP8X4), rhs_scale=eye_plane[:], start=True, stop=True)
+
+        def clock(ap):
+            tick = sb([P, 1], F32, f"tick{len(where)}")
+            nc.gpsimd.tensor_copy(out=tick[:], in_=ap)
+
+        def gather_scales(tile, first, j0, j1):
+            nc.vector.tensor_copy(tile[:, j0 - first : j1 - first], tab_plane[:].indirect(offsets[:, j0 // 16 : j1 // 16]))
 
         def second_tier(a, u):
             wr[a, u] = quantize(r_bf[a, u], NH, f"wr{a}{u}")
@@ -218,7 +247,8 @@ def tile_list_tiert_none_kernel(tc, tab_words, tab_scales, wt, x, wx_words, wx_s
                 codes, plane = tier[a, c // 2]
                 cols = slice(NC * (c % 2), NC * (c % 2 + 1))
             j0, j1 = SPANS[g]
-            scale = planes[0][4 * a : P, j0:j1]
+            first = 768 if g == 2 else 0
+            scale = planes[g // 2][4 * a : P, j0 - first : j1 - first]
             add_pass(c, g, 0, j1 - j0, codes[:, cols].bitcast(FP8X4), plane[:, cols], words[a, g][:].bitcast(FP8X4), scale)
 
         def x_pass(c, g):
@@ -237,6 +267,7 @@ def tile_list_tiert_none_kernel(tc, tab_words, tab_scales, wt, x, wx_words, wx_s
                 nc.vector.tensor_copy(out=res[:], in_=acc[i, g][:, 0:width])
             else:
                 nc.scalar.copy(out=res[:], in_=acc[i, g][:, 0:width])
+            results[i, g] = res
             if g == 1:
                 queue.dma_start(out[NH * i : NH * (i + 1), j0:j1].rearrange("(c p) j -> p c j", p=P), res[:].rearrange("p (c j) -> p c j", c=2))
             else:
@@ -250,50 +281,47 @@ def tile_list_tiert_none_kernel(tc, tab_words, tab_scales, wt, x, wx_words, wx_s
         nc.vector.memset(wx_plane[:].bitcast(I32), 0)
         make_eye()
         quantize_eye()
-        load_tab(nc.sync, 0)
         load_w(nc.sync, 0, 1)
+        load_tab(nc.sync, 0)
         load_w(nc.sync, 1, 0)
         load_w(nc.sync, 1, 1)
         load_tab(nc.sync, 1)
-        load_x(nc.sync, 0)
         for q in range(4):
             load_ws(nc.sync, q)
+        for s in range(4):
+            load_x(nc.sync, s)
         load_wxw(nc.sync)
-        load_x(nc.sync, 1)
-        load_x(nc.sync, 2)
-        load_x(nc.sync, 3)
         for a in range(2):
             for u in range(2):
                 cast_w(a, u)
         for s in range(4):
             cast_x(s)
-        gather_plane()
+        planes[0] = sb([P, 768], U8, "plane_early")
+        gather_scales(planes[0], 0, 0, 256)
         first_tier(0, 0)
         read_back(0, 0)
         read_back(0, 1)
-        gather_words(0, 0)
-        for c in (0, 1):
-            tab_pass(wq, 0, c, 0)
+        gather_scales(planes[0], 0, 256, 768)
         leftover(0, 0)
         leftover(0, 1)
         first_tier(0, 1)
         read_back(0, 2)
         read_back(0, 3)
-        for c in (2, 3):
+        gather_words(0, 0)
+        for c in range(4):
             tab_pass(wq, 0, c, 0)
-        gather_words(0, 1)
         second_tier(0, 0)
         for c in (0, 1):
             tab_pass(wr, 0, c, 0)
-        for c in (0, 1):
+        gather_words(0, 1)
+        for c in range(4):
             tab_pass(wq, 0, c, 1)
-            tab_pass(wr, 0, c, 1)
         leftover(0, 2)
         leftover(0, 3)
-        for c in (2, 3):
-            tab_pass(wq, 0, c, 1)
         first_tier(1, 0)
         read_back(1, 0)
+        for c in (0, 1):
+            tab_pass(wr, 0, c, 1)
         read_back(1, 1)
         first_tier(1, 1)
         second_tier(0, 1)
@@ -301,54 +329,60 @@ def tile_list_tiert_none_kernel(tc, tab_words, tab_scales, wt, x, wx_words, wx_s
             for c in (2, 3):
                 tab_pass(wr, 0, c, g)
         gather_words(1, 0)
-        for c in range(3):
+        for c in (0, 1):
             tab_pass(wq, 1, c, 0)
         leftover(1, 0)
         read_back(1, 2)
-        tab_pass(wq, 1, 3, 0)
+        for c in (2, 3):
+            tab_pass(wq, 1, c, 0)
         leftover(1, 1)
         read_back(1, 3)
-        quantize_x(0)
-        second_tier(1, 0)
-        for c in (0, 1):
-            tab_pass(wr, 1, c, 0)
-        quantize_x(1)
+        gather_words(1, 1)
         for c in range(4):
+            tab_pass(wq, 1, c, 1)
+        second_tier(1, 0)
+        for g in (0, 1):
+            for c in (0, 1):
+                tab_pass(wr, 1, c, g)
+        quantize_x(0)
+        quantize_x(1)
+        for c in (0, 1):
             x_pass(c, 0)
         store(0, 0, "scalar", nc.sync)
         store(1, 0, "scalar", nc.sync)
-        leftover_chunk(1, 2)
-        gather_words(1, 1)
-        for c in (0, 1):
-            tab_pass(wq, 1, c, 1)
-            tab_pass(wr, 1, c, 1)
-        second_tier_chunk(1, 2)
-        for c in (2, 3):
-            tab_pass(wq, 1, c, 1)
-        leftover_chunk(1, 3)
-        tab_pass(wr, 1, 2, 0)
-        store(2, 0, "scalar", nc.sync)
-        tab_pass(wr, 1, 2, 1)
-        gather_words(0, 2)
-        second_tier_chunk(1, 3)
-        for c in (0, 1):
-            tab_pass(wq, 0, c, 2)
-            tab_pass(wr, 0, c, 2)
-        tab_pass(wr, 1, 3, 0)
-        store(3, 0, "scalar", nc.sync)
+        leftover(1, 2)
         quantize_x(2)
         for c in (0, 1):
             x_pass(c, 1)
-        tab_pass(wr, 1, 3, 1)
+        store(0, 1, "scalar", nc.sync)
+        for g in (0, 1):
+            for c in (2, 3):
+                x_pass(c, g)
+        leftover(1, 3)
+        second_tier(1, 1)
         for c in (2, 3):
-            x_pass(c, 1)
+            tab_pass(wr, 1, c, 0)
+            store(c, 0, "scalar", nc.sync)
+        for c in (2, 3):
+            tab_pass(wr, 1, c, 1)
+        store(1, 1, "scalar", nc.sync)
+        planes[1] = sb([P, 256], U8, "plane_late")
+        gather_scales(planes[1], 768, 768, J)
+        gather_words(0, 2)
+        for c in (0, 1):
+            tab_pass(wq, 0, c, 2)
+            tab_pass(wr, 0, c, 2)
         gather_words(1, 2)
+        for c in (0, 1):
+            tab_pass(wq, 1, c, 2)
+            tab_pass(wr, 1, c, 2)
         quantize_x(3)
-        store(0, 1, "vector", nc.sync)
-        store(1, 1, "vector", nc.sync)
-        for c in range(4):
-            for a in range(2 if c > 1 else 1, 0, -1):
-                tab_pass(wq, 2 - a if c > 1 else 1, c, 2)
-                tab_pass(wr, 2 - a if c > 1 else 1, c, 2)
+        for c in (0, 1):
             x_pass(c, 2)
-            store(c, 2, "scalar", nc.sync)
+            store(c, 2, ("scalar", "vector")[c], nc.sync)
+        for c in (2, 3):
+            for a in range(2):
+                tab_pass(wq, a, c, 2)
+                tab_pass(wr, a, c, 2)
+            x_pass(c, 2)
+            store(c, 2, ("scalar", "vector")[c % 2], nc.sync)

@@ -24,12 +24,14 @@ NH = 256
 NC = 128
 SPANS = ((0, 512), (512, 768), (768, 1024))
 LATE_BANKS = ("shared0", "shared1", "bank0", "bank1")
-MARGINS = {}
+MARGINS = {"x_raw2": 2048, "w_bf00": 2048, "w_bf11": 2048}
 HOSTS = {
-    "plane_early": ("eye", 0), "wq00_codes": ("eye", 1024),
-    "wq01_codes": ("w_raw00", 0), "words00": ("w_raw00", 1024), "words01": ("w_raw00", 3072),
-    "words10": ("w_bf11", 0), "words11": ("w_raw10", 0), "r_bf11": ("x_raw1", 0),
-    "wr11_codes": ("x_raw3", 0), "plane_late": ("x_raw3", 1024), "words02": ("x_raw3", 2048), "words12": ("x_raw3", 3072),
+    "plane_early": ("eye", 0), "wq00_codes": ("eye", 1024), "w_bf01": ("w_bf00", 0),
+    "words00": ("w_bf00", -1984), "words01": ("w_bf00", 64),
+    "words10": ("w_bf11", -1984), "words11": ("w_bf11", 64),
+    "r_chunk12": ("x_raw0", 0), "wr10_plane": ("x_raw0", 1024), "r_chunk13": ("x_raw1", 0),
+    "res00": ("x_raw2", -1984), "plane_late": ("x_raw2", 64), "wr_chunk12_plane": ("x_raw2", 320), "wr_chunk13_plane": ("x_raw2", 448), "words02": ("x_raw2", 576), "words12": ("x_raw2", 1600), "res10": ("x_raw2", 2624),
+    "x_last0": ("r_chunk13", 0), "x_last1": ("r_chunk12", 0),
 }
 
 
@@ -219,6 +221,21 @@ def tile_list_tiert_none_kernel(tc, tab_words, tab_scales, wt, x, wx_words, wx_s
             cols = slice(JQ * s - j0, JQ * (s + 1) - j0)
             nc.vector.quantize_mx(out=codes[:, cols].bitcast(FP8X4), scales=plane[:, cols], in_=x_bf[s][:].rearrange("p w t -> p (w t)"))
 
+        def last_quarter():
+            halves = []
+            for h in range(2):
+                half = sb([P, NC, PACK], BF16, f"x_last{h}")
+                nc.vector.tensor_copy(out=woven(half[:]), in_=by_rows(x_raw[3][:, :, NC * h : NC * (h + 1)]))
+                halves.append(half)
+            xq[2] = (sb([P, JQ], U32, "xq2_codes"), sb([P, JQ], U8, "xq2_plane"))
+            for h in range(2):
+                cols = slice(NC * h, NC * (h + 1))
+                nc.vector.quantize_mx(out=xq[2][0][:, cols].bitcast(FP8X4), scales=xq[2][1][:, cols], in_=halves[h][:].rearrange("p w t -> p (w t)"))
+
+        def clock_words(ap):
+            tick = sb([P, 1], I32, f"tock{len(where)}")
+            nc.gpsimd.tensor_copy(out=tick[:], in_=ap.bitcast(I32))
+
         def bank(c, g):
             if g == 0:
                 key, tag, shape, first, count = (c, 0), f"bank{c}", [P, 512], 0, 5
@@ -288,24 +305,27 @@ def tile_list_tiert_none_kernel(tc, tab_words, tab_scales, wt, x, wx_words, wx_s
         load_tab(nc.sync, 1)
         for q in range(4):
             load_ws(nc.sync, q)
-        for s in range(4):
-            load_x(nc.sync, s)
+        load_x(nc.sync, 0)
         load_wxw(nc.sync)
+        load_x(nc.sync, 1)
+        load_x(nc.sync, 2)
+        load_x(nc.sync, 3)
         for a in range(2):
             for u in range(2):
                 cast_w(a, u)
-        for s in range(4):
+        for s in range(3):
             cast_x(s)
         planes[0] = sb([P, 768], U8, "plane_early")
         gather_scales(planes[0], 0, 0, 256)
         first_tier(0, 0)
         read_back(0, 0)
         read_back(0, 1)
+        warm_up(2)
         gather_scales(planes[0], 0, 256, 768)
         leftover(0, 0)
-        leftover(0, 1)
         first_tier(0, 1)
         read_back(0, 2)
+        leftover(0, 1)
         read_back(0, 3)
         gather_words(0, 0)
         for c in range(4):
@@ -329,43 +349,39 @@ def tile_list_tiert_none_kernel(tc, tab_words, tab_scales, wt, x, wx_words, wx_s
             for c in (2, 3):
                 tab_pass(wr, 0, c, g)
         gather_words(1, 0)
-        for c in (0, 1):
+        for c in range(4):
             tab_pass(wq, 1, c, 0)
+        gather_words(1, 1)
+        for c in (0, 1):
+            tab_pass(wq, 1, c, 1)
         leftover(1, 0)
         read_back(1, 2)
         for c in (2, 3):
-            tab_pass(wq, 1, c, 0)
+            tab_pass(wq, 1, c, 1)
         leftover(1, 1)
         read_back(1, 3)
-        gather_words(1, 1)
-        for c in range(4):
-            tab_pass(wq, 1, c, 1)
+        quantize_x(0)
         second_tier(1, 0)
         for g in (0, 1):
             for c in (0, 1):
                 tab_pass(wr, 1, c, g)
-        quantize_x(0)
+        leftover_chunk(1, 2)
         quantize_x(1)
-        for c in (0, 1):
+        for c in range(4):
             x_pass(c, 0)
         store(0, 0, "scalar", nc.sync)
         store(1, 0, "scalar", nc.sync)
-        leftover(1, 2)
-        quantize_x(2)
-        for c in (0, 1):
-            x_pass(c, 1)
-        store(0, 1, "scalar", nc.sync)
-        for g in (0, 1):
-            for c in (2, 3):
-                x_pass(c, g)
-        leftover(1, 3)
-        second_tier(1, 1)
+        leftover_chunk(1, 3)
+        second_tier_chunk(1, 2)
+        second_tier_chunk(1, 3)
         for c in (2, 3):
             tab_pass(wr, 1, c, 0)
             store(c, 0, "scalar", nc.sync)
         for c in (2, 3):
             tab_pass(wr, 1, c, 1)
-        store(1, 1, "scalar", nc.sync)
+        quantize_x(2)
+        for c in range(4):
+            x_pass(c, 1)
         planes[1] = sb([P, 256], U8, "plane_late")
         gather_scales(planes[1], 768, 768, J)
         gather_words(0, 2)
@@ -373,16 +389,20 @@ def tile_list_tiert_none_kernel(tc, tab_words, tab_scales, wt, x, wx_words, wx_s
             tab_pass(wq, 0, c, 2)
             tab_pass(wr, 0, c, 2)
         gather_words(1, 2)
+        store(0, 1, "scalar", nc.sync)
+        store(1, 1, "scalar", nc.sync)
         for c in (0, 1):
             tab_pass(wq, 1, c, 2)
             tab_pass(wr, 1, c, 2)
-        quantize_x(3)
-        for c in (0, 1):
-            x_pass(c, 2)
-            store(c, 2, ("scalar", "vector")[c], nc.sync)
-        for c in (2, 3):
-            for a in range(2):
-                tab_pass(wq, a, c, 2)
-                tab_pass(wr, a, c, 2)
+        for a in range(2):
+            tab_pass(wq, a, 2, 2)
+            tab_pass(wr, a, 2, 2)
+        last_quarter()
+        for c in range(3):
             x_pass(c, 2)
             store(c, 2, ("scalar", "vector")[c % 2], nc.sync)
+        for a in range(2):
+            tab_pass(wq, a, 3, 2)
+            tab_pass(wr, a, 3, 2)
+        x_pass(3, 2)
+        store(3, 2, "vector", nc.sync)

@@ -13,26 +13,48 @@ U16 = mybir.dt.uint16
 U8 = mybir.dt.uint8
 FP8X4 = mybir.dt.float8_e4m3fn_x4
 FP4X4 = mybir.dt.float4_e2m1fn_x4
-SUB = mybir.AluOpType.subtract
 BYTES_OF = {F32: 4, BF16: 2, I32: 4, U32: 4, U8: 1}
 
 P = 128
 PACK = 4
 KP = P * PACK
-JQ = 256
-NH = 256
-NC = 128
+CHUNK = 128
+HALF = 2 * CHUNK
+LOW, HIGH = (0, 1), (2, 3)
+QUARTER = J // 4
+BANK = 512
+PER_COLUMN = 16
 SPANS = ((0, 512), (512, 768), (768, 1024))
-LATE_BANKS = ("shared0", "shared1", "bank0", "bank1")
-MARGINS = {"x_raw2": 2048, "w_bf00": 2048, "w_bf11": 2048}
-HOSTS = {
-    "plane_early": ("eye", 0), "wq00_codes": ("eye", 1024), "w_bf01": ("w_bf00", 0),
-    "words00": ("w_bf00", -1984), "words01": ("w_bf00", 64),
-    "words10": ("w_bf11", -1984), "words11": ("w_bf11", 64),
-    "r_chunk12": ("x_raw0", 0), "wr10_plane": ("x_raw0", 1024), "r_chunk13": ("x_raw1", 0),
-    "res00": ("x_raw2", -1984), "plane_late": ("x_raw2", 64), "wr_chunk12_plane": ("x_raw2", 320), "wr_chunk13_plane": ("x_raw2", 448), "words02": ("x_raw2", 576), "words12": ("x_raw2", 1600), "res10": ("x_raw2", 2624),
-    "x_last0": ("r_chunk13", 0), "x_last1": ("r_chunk12", 0),
+EARLY = SPANS[1][1]
+FIRST_SCALES = 256
+LATE_BANKS = ("back0", "back1", "bank0", "bank1")
+NARROW = 128
+ALIGN = 64
+
+LEAD = ALIGN - 2048
+PLACED_ON = {
+    "scales_early": ("eye", 0),
+    "wq00_codes": ("eye", 1024),
+    "w_bf01": ("w_bf00", 0),
+    "words00": ("w_bf00", LEAD),
+    "words01": ("w_bf00", ALIGN),
+    "words10": ("w_bf11", LEAD),
+    "words11": ("w_bf11", ALIGN),
+    "rest12": ("x_raw0", 0),
+    "wr10_plane": ("x_raw0", 1024),
+    "rest13": ("x_raw1", 0),
+    "result00": ("x_raw2", LEAD),
+    "scales_late": ("x_raw2", ALIGN),
+    "wr12_plane": ("x_raw2", ALIGN + 256),
+    "wr13_plane": ("x_raw2", ALIGN + 384),
+    "words02": ("x_raw2", ALIGN + 512),
+    "words12": ("x_raw2", ALIGN + 1536),
+    "result10": ("x_raw2", ALIGN + 2560),
+    "x_last0": ("rest13", 0),
+    "x_last1": ("rest12", 0),
 }
+MARGIN = 2048
+WITH_MARGIN = ("w_bf00", "w_bf11", "x_raw2")
 
 
 def woven(ap):
@@ -49,22 +71,22 @@ def tile_list_tiert_none_kernel(tc, tab_words, tab_scales, wt, x, wx_words, wx_s
         keep = ctx.enter_context(tc.tile_pool(name="keep", bufs=1))
         work = ctx.enter_context(tc.tile_pool(name="work", bufs=1))
         psum = ctx.enter_context(tc.psum_pool(name="psum", bufs=1))
-        where = {"end": 0}
+        start_of = {"free": 0}
 
         def sb(shape, dtype, name):
             size = BYTES_OF[dtype]
             for extent in shape[1:]:
                 size = size * extent
-            if name in HOSTS:
-                host, inside = HOSTS[name]
-                where[name] = where[host] + inside
+            if name in PLACED_ON:
+                spent, inside = PLACED_ON[name]
+                start_of[name] = start_of[spent] + inside
             else:
-                margin = MARGINS.get(name, 0)
-                where[name] = where["end"] + margin
-                where["end"] = where[name] + (size + 63) // 64 * 64 + margin
-            return work.tile(shape, dtype, name=name, align_bytes=64, offset=where[name])
+                margin = MARGIN if name in WITH_MARGIN else 0
+                start_of[name] = start_of["free"] + margin
+                start_of["free"] = start_of[name] + (size + ALIGN - 1) // ALIGN * ALIGN + margin
+            return work.tile(shape, dtype, name=name, align_bytes=ALIGN, offset=start_of[name])
 
-        offsets = keep.tile([P, J // 16], U16, name="offsets")
+        offsets = keep.tile([P, J // PER_COLUMN], U16, name="offsets")
         tab_plane = sb([P, T], U8, "tab_plane")
         wx_plane = sb([P, N], U8, "wx_plane")
         wx_codes = sb([P, 2 * N], U8, "wx_codes")
@@ -73,336 +95,270 @@ def tile_list_tiert_none_kernel(tc, tab_words, tab_scales, wt, x, wx_words, wx_s
         eye_codes = sb([P, KP], U32, "eye_codes")
         eye_plane = sb([P, KP], U8, "eye_plane")
         w_raw, w_bf, tab_raw, x_raw, x_bf = {}, {}, {}, {}, {}
-        planes, words, wq, wr, xq, acc, back, r_bf = {}, {}, {}, {}, {}, {}, {}, {}
-        done, parked, results = {}, {}, {}
+        wq, wr, rest, back, words, xq = {}, {}, {}, {}, {}, {}
+        sums, passes_done = {}, {}
 
-        def load_ts(eng, q):
-            eng.dma_start(tab_plane[32 * q : 32 * q + 8, :].bitcast(I32), tab_scales[:, 4 * q : 4 * q + 4, :].bitcast(I32))
+        def listed(j0, j1):
+            return offsets[:, j0 // PER_COLUMN : j1 // PER_COLUMN]
 
-        def load_ws(eng, q):
-            eng.dma_start(wx_plane[32 * q : 32 * q + 4, :].bitcast(I32), wx_scales[0, 4 * q : 4 * q + 4, :].bitcast(I32))
+        def load_w(a, u):
+            w_raw[a, u] = sb([P, PACK, HALF], F32, f"w_raw{a}{u}")
+            rows = wt[KP * a : KP * (a + 1), HALF * u : HALF * (u + 1)]
+            nc.sync.dma_start(w_raw[a, u][:], rows.rearrange("(p t) n -> p t n", t=PACK))
 
-        def load_wxw(eng):
-            eng.dma_start(wx_codes[:].bitcast(I32), wx_words[0].bitcast(I32))
-
-        def load_w(eng, a, u):
-            w_raw[a, u] = sb([P, PACK, NH], F32, f"w_raw{a}{u}")
-            eng.dma_start(w_raw[a, u][:], wt[KP * a : KP * (a + 1), NH * u : NH * (u + 1)].rearrange("(p j) n -> p j n", j=PACK))
-
-        def load_w_pass(eng, a):
-            whole = sb([P, PACK, N], F32, f"w_raw{a}")
-            eng.dma_start(whole[:], wt[KP * a : KP * (a + 1), :].rearrange("(p j) n -> p j n", j=PACK))
-            for u in range(2):
-                w_raw[a, u] = whole[:, :, NH * u : NH * (u + 1)]
-
-        def load_x_half(eng, h):
-            half = sb([P, PACK, 2 * JQ], F32, f"x_half{h}")
-            eng.dma_start(half[:], x[:, 2 * JQ * h : 2 * JQ * (h + 1)].rearrange("(p j) w -> p j w", j=PACK))
-            for s in range(2):
-                x_raw[2 * h + s] = half[:, :, JQ * s : JQ * (s + 1)]
-
-        def load_tab(eng, a):
+        def load_table(a):
             tab_raw[a] = sb([P, T], I32, f"tab_raw{a}")
-            eng.dma_start(tab_raw[a][:], tab_words[a].rearrange("p t i -> p (t i)").bitcast(I32))
+            nc.sync.dma_start(tab_raw[a][:], tab_words[a].rearrange("p c t -> p (c t)").bitcast(I32))
 
-        def load_x(eng, s):
-            x_raw[s] = sb([P, PACK, JQ], F32, f"x_raw{s}")
-            eng.dma_start(x_raw[s][:], x[:, JQ * s : JQ * (s + 1)].rearrange("(p j) w -> p j w", j=PACK))
+        def load_x(s):
+            x_raw[s] = sb([P, PACK, QUARTER], F32, f"x_raw{s}")
+            nc.sync.dma_start(x_raw[s][:], x[:, QUARTER * s : QUARTER * (s + 1)].rearrange("(p t) j -> p t j", t=PACK))
 
-        def make_eye():
+        def make_identity_operand():
             nc.gpsimd.iota(ramp[:], pattern=[[1, KP // 2]], base=P, channel_multiplier=-PACK, allow_small_or_imprecise_dtypes=True)
             for t in range(PACK):
                 for h in range(2):
                     first = KP * t + KP // 2 * h
-                    nc.vector.tensor_scalar(out=eye[:, first : first + KP // 2], in0=ramp[:], scalar1=float(P + t - KP // 2 * h), scalar2=None, op0=mybir.AluOpType.is_equal)
+                    nc.vector.tensor_scalar(
+                        out=eye[:, first : first + KP // 2], in0=ramp[:], scalar1=float(P + t - KP // 2 * h), scalar2=None, op0=mybir.AluOpType.is_equal
+                    )
+            nc.vector.quantize_mx(out=eye_codes[:].bitcast(FP8X4), scales=eye_plane[:], in_=eye[:])
 
-        def quantize_eye():
-            nc.vector.quantize_mx(out=eye_codes[:].bitcast(FP8X4), scales=eye_plane[:], in_=eye[:, 0 : 4 * KP])
-
-        def gather_plane(h):
-            planes[h] = sb([P, J // 2], U8, f"plane{h}")
-            nc.vector.tensor_copy(planes[h][:], tab_plane[:].indirect(offsets[:, 32 * h : 32 * (h + 1)]))
-
+        def gather_scales(tile, first, j0, j1):
+            nc.vector.tensor_copy(tile[:, j0 - first : j1 - first], tab_plane[:].indirect(listed(j0, j1)))
 
         def gather_words(a, g):
             j0, j1 = SPANS[g]
             words[a, g] = sb([P, j1 - j0], U32, f"words{a}{g}")
-            nc.vector.tensor_copy(words[a, g][:], tab_raw[a][:].bitcast(U32).indirect(offsets[:, j0 // 16 : j1 // 16]))
+            nc.vector.tensor_copy(words[a, g][:], tab_raw[a][:].bitcast(U32).indirect(listed(j0, j1)))
 
-        def quantize(grouped, width, name):
-            codes = sb([P, width], U32, name + "_codes")
-            plane = sb([P, width], U8, name + "_plane")
-            nc.vector.quantize_mx(out=codes[:].bitcast(FP8X4), scales=plane[:], in_=grouped[:].rearrange("p w t -> p (w t)"))
-            return codes, plane
+        def mx_tiles(width, name):
+            return sb([P, width], U32, name + "_codes"), sb([P, width], U8, name + "_plane")
+
+        def quantize(operand, cols, grouped):
+            codes, plane = operand
+            nc.vector.quantize_mx(out=codes[:, cols].bitcast(FP8X4), scales=plane[:, cols], in_=grouped[:].rearrange("p c t -> p (c t)"))
 
         def cast_w(a, u):
-            w_bf[a, u] = sb([P, NH, PACK], BF16, f"w_bf{a}{u}")
+            w_bf[a, u] = sb([P, HALF, PACK], BF16, f"w_bf{a}{u}")
             nc.scalar.copy(out=woven(w_bf[a, u][:]), in_=by_rows(w_raw[a, u][:]))
 
+        def cast_x(s):
+            x_bf[s] = sb([P, QUARTER, PACK], BF16, f"x_bf{s}")
+            nc.scalar.copy(out=woven(x_bf[s][:]), in_=by_rows(x_raw[s][:]))
+
+        def by_chunk(tier, a, chunks, operand):
+            codes, plane = operand
+            for i, c in enumerate(chunks):
+                cols = slice(CHUNK * i, CHUNK * (i + 1))
+                tier[a, c] = (codes[:, cols].bitcast(FP8X4), plane[:, cols])
+
         def first_tier(a, u):
-            wq[a, u] = quantize(w_bf[a, u], NH, f"wq{a}{u}")
+            operand = mx_tiles(HALF, f"wq{a}{u}")
+            quantize(operand, slice(0, HALF), w_bf[a, u])
+            by_chunk(wq, a, (2 * u, 2 * u + 1), operand)
 
         def read_back(a, c):
-            codes, plane = wq[a, c // 2]
-            cols = slice(NC * (c % 2), NC * (c % 2 + 1))
-            back[a, c] = psum.tile([P, PACK, NC], F32, name="back", tag=f"shared{c % 2}")
+            codes, plane = wq[a, c]
+            back[a, c] = psum.tile([P, PACK, CHUNK], F32, name="back", tag=f"back{c % 2}")
             for t in range(PACK):
                 nc.tensor.matmul_mx(
                     out=back[a, c][:, t, :],
                     lhsT=eye_codes[:, P * t : P * (t + 1)].bitcast(FP8X4),
                     lhsT_scale=eye_plane[:, P * t : P * (t + 1)],
-                    rhs=codes[:, cols].bitcast(FP8X4),
-                    rhs_scale=plane[:, cols],
+                    rhs=codes,
+                    rhs_scale=plane,
                     start=True,
                     stop=True,
                 )
 
-        def leftover(a, c):
-            u = c // 2
-            cols = slice(NC * (c % 2), NC * (c % 2 + 1))
-            if (a, u) not in r_bf:
-                r_bf[a, u] = sb([P, NH, PACK], BF16, f"r_bf{a}{u}")
-            nc.vector.tensor_tensor(out=woven(r_bf[a, u][:, cols, :]), in0=by_rows(w_raw[a, u][:, :, cols]), in1=by_rows(back[a, c][:]), op=SUB)
+        def subtract(a, c, chunks):
+            if (a, chunks) not in rest:
+                rest[a, chunks] = sb([P, CHUNK * len(chunks), PACK], BF16, f"rest{a}{chunks[0]}")
+            place = CHUNK * chunks.index(c)
+            own = slice(CHUNK * (c % 2), CHUNK * (c % 2 + 1))
+            nc.vector.tensor_tensor(
+                out=woven(rest[a, chunks][:, place : place + CHUNK, :]),
+                in0=by_rows(w_raw[a, c // 2][:, :, own]),
+                in1=by_rows(back[a, c][:]),
+                op=mybir.AluOpType.subtract,
+            )
 
-        def park(a, c):
-            parked[a, c] = sb([P, NC, PACK], F32, f"parked{a}{c}")
-            nc.scalar.copy(out=parked[a, c][:], in_=back[a, c][:].rearrange("p t n -> p n t"))
-
-        def leftover_pool(a, c):
-            u = c // 2
-            cols = slice(NC * (c % 2), NC * (c % 2 + 1))
-            if (a, u) not in r_bf:
-                r_bf[a, u] = sb([P, NH, PACK], BF16, f"r_bf{a}{u}")
-            nc.gpsimd.tensor_tensor(out=r_bf[a, u][:, cols, :], in0=w_raw[a, u][:, :, cols].rearrange("p t n -> p n t"), in1=parked[a, c][:], op=SUB)
-
-        def gather_planes():
-            whole = sb([P, J], U8, "plane")
-            nc.vector.tensor_copy(whole[:], tab_plane[:].indirect(offsets[:]))
-            planes[0], planes[1] = whole[:, 0:512], whole[:, 512:J]
-
-        def warm_up(count):
-            spare = psum.tile([P, KP], F32, name="spare", tag="bank3")
-            codes, plane = wq[0, 0]
-            for i in range(count):
-                nc.tensor.matmul_mx(out=spare[:], lhsT=codes[:, 0:NC].bitcast(FP8X4), lhsT_scale=plane[:, 0:NC],
-                                    rhs=eye_codes[:].bitcast(FP8X4), rhs_scale=eye_plane[:], start=True, stop=True)
-
-        def clock(ap):
-            tick = sb([P, 1], F32, f"tick{len(where)}")
-            nc.gpsimd.tensor_copy(out=tick[:], in_=ap)
-
-        def gather_scales(tile, first, j0, j1):
-            nc.vector.tensor_copy(tile[:, j0 - first : j1 - first], tab_plane[:].indirect(offsets[:, j0 // 16 : j1 // 16]))
-
-        def second_tier(a, u):
-            wr[a, u] = quantize(r_bf[a, u], NH, f"wr{a}{u}")
-
-        def leftover_chunk(a, c):
-            cols = slice(NC * (c % 2), NC * (c % 2 + 1))
-            r_bf[a, "chunk", c] = sb([P, NC, PACK], BF16, f"r_chunk{a}{c}")
-            nc.vector.tensor_tensor(out=woven(r_bf[a, "chunk", c][:]), in0=by_rows(w_raw[a, c // 2][:, :, cols]), in1=by_rows(back[a, c][:]), op=SUB)
-
-        def second_tier_chunk(a, c):
-            wr[a, "chunk", c] = quantize(r_bf[a, "chunk", c], NC, f"wr_chunk{a}{c}")
-
-        def cast_x(s, eng="scalar"):
-            x_bf[s] = sb([P, JQ, PACK], BF16, f"x_bf{s}")
-            if eng == "vector":
-                nc.vector.tensor_copy(out=woven(x_bf[s][:]), in_=by_rows(x_raw[s][:]))
-            else:
-                nc.scalar.copy(out=woven(x_bf[s][:]), in_=by_rows(x_raw[s][:]))
+        def second_tier(a, chunks):
+            width = CHUNK * len(chunks)
+            operand = mx_tiles(width, f"wr{a}{chunks[0]}")
+            quantize(operand, slice(0, width), rest[a, chunks])
+            by_chunk(wr, a, chunks, operand)
 
         def quantize_x(s):
-            g = max(s - 1, 0)
+            g = s // 2
             j0, j1 = SPANS[g]
             if g not in xq:
-                xq[g] = (sb([P, j1 - j0], U32, f"xq{g}_codes"), sb([P, j1 - j0], U8, f"xq{g}_plane"))
-            codes, plane = xq[g]
-            cols = slice(JQ * s - j0, JQ * (s + 1) - j0)
-            nc.vector.quantize_mx(out=codes[:, cols].bitcast(FP8X4), scales=plane[:, cols], in_=x_bf[s][:].rearrange("p w t -> p (w t)"))
+                xq[g] = mx_tiles(j1 - j0, f"xq{g}")
+            quantize(xq[g], slice(QUARTER * s - j0, QUARTER * (s + 1) - j0), x_bf[s])
 
-        def last_quarter():
-            halves = []
+        def last_quarter_of_x():
+            parts = []
             for h in range(2):
-                half = sb([P, NC, PACK], BF16, f"x_last{h}")
-                nc.vector.tensor_copy(out=woven(half[:]), in_=by_rows(x_raw[3][:, :, NC * h : NC * (h + 1)]))
-                halves.append(half)
-            xq[2] = (sb([P, JQ], U32, "xq2_codes"), sb([P, JQ], U8, "xq2_plane"))
+                part = sb([P, NARROW, PACK], BF16, f"x_last{h}")
+                nc.vector.tensor_copy(out=woven(part[:]), in_=by_rows(x_raw[3][:, :, NARROW * h : NARROW * (h + 1)]))
+                parts.append(part)
+            xq[2] = mx_tiles(QUARTER, "xq2")
             for h in range(2):
-                cols = slice(NC * h, NC * (h + 1))
-                nc.vector.quantize_mx(out=xq[2][0][:, cols].bitcast(FP8X4), scales=xq[2][1][:, cols], in_=halves[h][:].rearrange("p w t -> p (w t)"))
-
-        def clock_words(ap):
-            tick = sb([P, 1], I32, f"tock{len(where)}")
-            nc.gpsimd.tensor_copy(out=tick[:], in_=ap.bitcast(I32))
-
-        def bank(c, g):
-            if g == 0:
-                key, tag, shape, first, count = (c, 0), f"bank{c}", [P, 512], 0, 5
-            elif g == 1:
-                key, tag, shape, first, count = (c // 2, 1), f"bank{4 + c // 2}", [P, 512], JQ * (c % 2), 12
-            else:
-                key, tag, shape, first, count = (c, 2), LATE_BANKS[c], [P, 512], 0, 6
-            if key not in acc:
-                acc[key] = psum.tile(shape, F32, name=f"acc{key[0]}{key[1]}", tag=tag)
-                done[key] = 0
-            return key, first, count
+                quantize(xq[2], slice(NARROW * h, NARROW * (h + 1)), parts[h])
 
         def add_pass(c, g, j0, j1, lhsT, lhsT_scale, rhs, rhs_scale):
-            key, first, count = bank(c, g)
-            nc.tensor.matmul_mx(
-                out=acc[key][:, first + j0 : first + j1], lhsT=lhsT, lhsT_scale=lhsT_scale, rhs=rhs, rhs_scale=rhs_scale,
-                start=(done[key] == 0), stop=(done[key] == count - 1),
-            )
-            done[key] = done[key] + 1
-
-        def tab_pass(tier, a, c, g):
-            if (a, "chunk", c) in tier:
-                codes, plane = tier[a, "chunk", c]
-                cols = slice(0, NC)
+            if g == 0:
+                key, tag, first, count = (c, g), f"bank{c}", 0, 5
+            elif g == 1:
+                key, tag, first, count = (c // 2, g), f"bank{4 + c // 2}", QUARTER * (c % 2), 12
             else:
-                codes, plane = tier[a, c // 2]
-                cols = slice(NC * (c % 2), NC * (c % 2 + 1))
-            j0, j1 = SPANS[g]
-            first = 768 if g == 2 else 0
-            scale = planes[g // 2][4 * a : P, j0 - first : j1 - first]
-            add_pass(c, g, 0, j1 - j0, codes[:, cols].bitcast(FP8X4), plane[:, cols], words[a, g][:].bitcast(FP8X4), scale)
+                key, tag, first, count = (c, g), LATE_BANKS[c], 0, 6
+            if key not in sums:
+                sums[key] = psum.tile([P, BANK], F32, name=f"sum{key[0]}{key[1]}", tag=tag)
+                passes_done[key] = 0
+            nc.tensor.matmul_mx(
+                out=sums[key][:, first + j0 : first + j1],
+                lhsT=lhsT,
+                lhsT_scale=lhsT_scale,
+                rhs=rhs,
+                rhs_scale=rhs_scale,
+                start=(passes_done[key] == 0),
+                stop=(passes_done[key] == count - 1),
+            )
+            passes_done[key] = passes_done[key] + 1
 
-        def x_pass(c, g):
+        def table_passes(tier, a, chunks, g):
+            j0, j1 = SPANS[g]
+            scales = scales_late[PACK * a : P, :] if g == 2 else scales_early[PACK * a : P, j0:j1]
+            for c in chunks:
+                codes, plane = tier[a, c]
+                add_pass(c, g, 0, j1 - j0, codes, plane, words[a, g][:].bitcast(FP8X4), scales)
+
+        def both_tiers(a, c, g):
+            table_passes(wq, a, (c,), g)
+            table_passes(wr, a, (c,), g)
+
+        def x_passes(chunks, g):
             codes, plane = xq[g]
             j0, j1 = SPANS[g]
-            step = 512 if g == 0 else 128
-            for k in range(0, j1 - j0, step):
-                add_pass(c, g, k, k + step, wx_codes[:, 2 * NC * c : 2 * NC * (c + 1)].bitcast(FP4X4), wx_plane[:, NC * c : NC * (c + 1)],
-                         codes[:, k : k + step].bitcast(FP8X4), plane[:, k : k + step])
+            width = BANK if g == 0 else NARROW
+            for c in chunks:
+                stationary = wx_codes[:, 2 * CHUNK * c : 2 * CHUNK * (c + 1)].bitcast(FP4X4)
+                for j in range(0, j1 - j0, width):
+                    add_pass(c, g, j, j + width, stationary, wx_plane[:, CHUNK * c : CHUNK * (c + 1)], codes[:, j : j + width].bitcast(FP8X4), plane[:, j : j + width])
 
-        def store(i, g, eng, queue):
+        def store(i, g, on_vector):
             j0, j1 = SPANS[g]
-            width = 256 if g == 2 else 512
-            res = sb([P, width], F32, f"res{i}{g}")
-            if eng == "vector":
-                nc.vector.tensor_copy(out=res[:], in_=acc[i, g][:, 0:width])
+            width = QUARTER if g == 2 else BANK
+            result = sb([P, width], F32, f"result{i}{g}")
+            if on_vector:
+                nc.vector.tensor_copy(out=result[:], in_=sums[i, g][:, 0:width])
             else:
-                nc.scalar.copy(out=res[:], in_=acc[i, g][:, 0:width])
-            results[i, g] = res
+                nc.scalar.copy(out=result[:], in_=sums[i, g][:, 0:width])
             if g == 1:
-                queue.dma_start(out[NH * i : NH * (i + 1), j0:j1].rearrange("(c p) j -> p c j", p=P), res[:].rearrange("p (c j) -> p c j", c=2))
+                rows = out[HALF * i : HALF * (i + 1), j0:j1].rearrange("(c p) j -> p c j", p=P)
+                nc.sync.dma_start(rows, result[:].rearrange("p (c j) -> p c j", c=2))
             else:
-                queue.dma_start(out[NC * i : NC * (i + 1), j0:j1], res[:])
+                nc.sync.dma_start(out[CHUNK * i : CHUNK * (i + 1), j0:j1], result[:])
 
         nc.vector.memset(tab_plane[:].bitcast(I32), 0)
-        load_w(nc.sync, 0, 0)
+        load_w(0, 0)
         nc.sync.dma_start(offsets[:], offs)
         for q in range(4):
-            load_ts(nc.sync, q)
+            nc.sync.dma_start(tab_plane[32 * q : 32 * q + 8, :].bitcast(I32), tab_scales[:, 4 * q : 4 * q + 4, :].bitcast(I32))
         nc.vector.memset(wx_plane[:].bitcast(I32), 0)
-        make_eye()
-        quantize_eye()
-        load_w(nc.sync, 0, 1)
-        load_tab(nc.sync, 0)
-        load_w(nc.sync, 1, 0)
-        load_w(nc.sync, 1, 1)
-        load_tab(nc.sync, 1)
+        make_identity_operand()
+        load_w(0, 1)
+        load_table(0)
+        load_w(1, 0)
+        load_w(1, 1)
+        load_table(1)
         for q in range(4):
-            load_ws(nc.sync, q)
-        load_x(nc.sync, 0)
-        load_wxw(nc.sync)
-        load_x(nc.sync, 1)
-        load_x(nc.sync, 2)
-        load_x(nc.sync, 3)
+            nc.sync.dma_start(wx_plane[32 * q : 32 * q + 4, :].bitcast(I32), wx_scales[0, 4 * q : 4 * q + 4, :].bitcast(I32))
+        load_x(0)
+        nc.sync.dma_start(wx_codes[:].bitcast(I32), wx_words[0].bitcast(I32))
+        for s in range(1, 4):
+            load_x(s)
         for a in range(2):
             for u in range(2):
                 cast_w(a, u)
         for s in range(3):
             cast_x(s)
-        planes[0] = sb([P, 768], U8, "plane_early")
-        gather_scales(planes[0], 0, 0, 256)
+
+        scales_early = sb([P, EARLY], U8, "scales_early")
+        gather_scales(scales_early, 0, 0, FIRST_SCALES)
         first_tier(0, 0)
         read_back(0, 0)
         read_back(0, 1)
-        warm_up(2)
-        gather_scales(planes[0], 0, 256, 768)
-        leftover(0, 0)
+        gather_scales(scales_early, 0, FIRST_SCALES, EARLY)
+        subtract(0, 0, LOW)
         first_tier(0, 1)
         read_back(0, 2)
-        leftover(0, 1)
+        subtract(0, 1, LOW)
         read_back(0, 3)
         gather_words(0, 0)
-        for c in range(4):
-            tab_pass(wq, 0, c, 0)
-        second_tier(0, 0)
-        for c in (0, 1):
-            tab_pass(wr, 0, c, 0)
+        table_passes(wq, 0, range(4), 0)
+        second_tier(0, LOW)
+        table_passes(wr, 0, LOW, 0)
         gather_words(0, 1)
-        for c in range(4):
-            tab_pass(wq, 0, c, 1)
-        leftover(0, 2)
-        leftover(0, 3)
+        table_passes(wq, 0, range(4), 1)
+        subtract(0, 2, HIGH)
+        subtract(0, 3, HIGH)
         first_tier(1, 0)
         read_back(1, 0)
-        for c in (0, 1):
-            tab_pass(wr, 0, c, 1)
+        table_passes(wr, 0, LOW, 1)
         read_back(1, 1)
         first_tier(1, 1)
-        second_tier(0, 1)
-        for g in (0, 1):
-            for c in (2, 3):
-                tab_pass(wr, 0, c, g)
+        second_tier(0, HIGH)
+        for g in range(2):
+            table_passes(wr, 0, HIGH, g)
+
         gather_words(1, 0)
-        for c in range(4):
-            tab_pass(wq, 1, c, 0)
+        table_passes(wq, 1, range(4), 0)
         gather_words(1, 1)
-        for c in (0, 1):
-            tab_pass(wq, 1, c, 1)
-        leftover(1, 0)
+        table_passes(wq, 1, LOW, 1)
+        subtract(1, 0, LOW)
         read_back(1, 2)
-        for c in (2, 3):
-            tab_pass(wq, 1, c, 1)
-        leftover(1, 1)
+        table_passes(wq, 1, HIGH, 1)
+        subtract(1, 1, LOW)
         read_back(1, 3)
         quantize_x(0)
-        second_tier(1, 0)
-        for g in (0, 1):
-            for c in (0, 1):
-                tab_pass(wr, 1, c, g)
-        leftover_chunk(1, 2)
+        second_tier(1, LOW)
+        for g in range(2):
+            table_passes(wr, 1, LOW, g)
+        subtract(1, 2, (2,))
         quantize_x(1)
-        for c in range(4):
-            x_pass(c, 0)
-        store(0, 0, "scalar", nc.sync)
-        store(1, 0, "scalar", nc.sync)
-        leftover_chunk(1, 3)
-        second_tier_chunk(1, 2)
-        second_tier_chunk(1, 3)
-        for c in (2, 3):
-            tab_pass(wr, 1, c, 0)
-            store(c, 0, "scalar", nc.sync)
-        for c in (2, 3):
-            tab_pass(wr, 1, c, 1)
+        x_passes(range(4), 0)
+        store(0, 0, False)
+        store(1, 0, False)
+        subtract(1, 3, (3,))
+        for c in HIGH:
+            second_tier(1, (c,))
+        for c in HIGH:
+            table_passes(wr, 1, (c,), 0)
+            store(c, 0, False)
+        table_passes(wr, 1, HIGH, 1)
         quantize_x(2)
-        for c in range(4):
-            x_pass(c, 1)
-        planes[1] = sb([P, 256], U8, "plane_late")
-        gather_scales(planes[1], 768, 768, J)
+        x_passes(range(4), 1)
+
+        scales_late = sb([P, J - EARLY], U8, "scales_late")
+        gather_scales(scales_late, EARLY, EARLY, J)
         gather_words(0, 2)
-        for c in (0, 1):
-            tab_pass(wq, 0, c, 2)
-            tab_pass(wr, 0, c, 2)
+        for c in LOW:
+            both_tiers(0, c, 2)
         gather_words(1, 2)
-        store(0, 1, "scalar", nc.sync)
-        store(1, 1, "scalar", nc.sync)
-        for c in (0, 1):
-            tab_pass(wq, 1, c, 2)
-            tab_pass(wr, 1, c, 2)
+        store(0, 1, False)
+        store(1, 1, False)
+        for c in LOW:
+            both_tiers(1, c, 2)
         for a in range(2):
-            tab_pass(wq, a, 2, 2)
-            tab_pass(wr, a, 2, 2)
-        last_quarter()
+            both_tiers(a, 2, 2)
+        last_quarter_of_x()
         for c in range(3):
-            x_pass(c, 2)
-            store(c, 2, ("scalar", "vector")[c % 2], nc.sync)
+            x_passes((c,), 2)
+            store(c, 2, c % 2 == 1)
         for a in range(2):
-            tab_pass(wq, a, 3, 2)
-            tab_pass(wr, a, 3, 2)
-        x_pass(3, 2)
-        store(3, 2, "vector", nc.sync)
+            both_tiers(a, 3, 2)
+        x_passes((3,), 2)
+        store(3, 2, True)

@@ -21,40 +21,36 @@ KP = P * PACK
 CHUNK = 128
 HALF = 2 * CHUNK
 LOW, HIGH = (0, 1), (2, 3)
+ALL = (0, 1, 2, 3)
 QUARTER = J // 4
 BANK = 512
 PER_COLUMN = 16
 SPANS = ((0, 512), (512, 768), (768, 1024))
-EARLY = SPANS[1][1]
-FIRST_SCALES = 256
 LATE_BANKS = ("back0", "back1", "bank0", "bank1")
-NARROW = 128
 ALIGN = 64
-
-LEAD = ALIGN - 2048
-PLACED_ON = {
-    "scales_early": ("eye", 0),
-    "wq00_codes": ("eye", 1024),
-    "w_bf01": ("w_bf00", 0),
-    "words00": ("w_bf00", LEAD),
-    "words01": ("w_bf00", ALIGN),
-    "words10": ("w_bf11", LEAD),
-    "words11": ("w_bf11", ALIGN),
-    "rest12": ("x_raw0", 0),
-    "wr10_plane": ("x_raw0", 1024),
-    "rest13": ("x_raw1", 0),
-    "result00": ("x_raw2", LEAD),
-    "scales_late": ("x_raw2", ALIGN),
-    "wr12_plane": ("x_raw2", ALIGN + 256),
-    "wr13_plane": ("x_raw2", ALIGN + 384),
-    "words02": ("x_raw2", ALIGN + 512),
-    "words12": ("x_raw2", ALIGN + 1536),
-    "result10": ("x_raw2", ALIGN + 2560),
-    "x_last0": ("rest13", 0),
-    "x_last1": ("rest12", 0),
-}
+SHARE = 64
 MARGIN = 2048
-WITH_MARGIN = ("w_bf00", "w_bf11", "x_raw2")
+
+PLACED_ON = {
+    "scales0": "eye",
+    "wq00_codes": "eye",
+    "w_bf02": "w_bf00",
+    "words00": "w_bf02",
+    "words01": "w_raw00",
+    "words10": "w_bf12",
+    "words11": "w_bf12",
+    "rest12": "x_raw0",
+    "wr10_plane": "x_raw0",
+    "wr12_plane": "x_raw1",
+    "rest13": "x_raw1",
+    "result00": "x_raw2",
+    "result10": "x_raw2",
+    "scales768": "rest12",
+    "words02": "rest13",
+    "words12": "x_bf2",
+    "x_last0": "x_bf2",
+    "x_last1": "x_raw2",
+}
 
 
 def woven(ap):
@@ -71,20 +67,33 @@ def tile_list_tiert_none_kernel(tc, tab_words, tab_scales, wt, x, wx_words, wx_s
         keep = ctx.enter_context(tc.tile_pool(name="keep", bufs=1))
         work = ctx.enter_context(tc.tile_pool(name="work", bufs=1))
         psum = ctx.enter_context(tc.psum_pool(name="psum", bufs=1))
-        start_of = {"free": 0}
+        hosts = set(PLACED_ON.values())
+        free = {"fresh": 0}
+        end_of = {}
 
         def sb(shape, dtype, name):
             size = BYTES_OF[dtype]
             for extent in shape[1:]:
                 size = size * extent
+            size = (size + ALIGN - 1) // ALIGN * ALIGN
             if name in PLACED_ON:
-                spent, inside = PLACED_ON[name]
-                start_of[name] = start_of[spent] + inside
+                spent = PLACED_ON[name]
+                start = free[spent]
+                if (spent, "first") in free:
+                    start = free.pop((spent, "first")) - size
+                else:
+                    assert start < end_of[spent] and start + size <= end_of[spent] + (0 if spent in PLACED_ON else MARGIN), name
+                    free[spent] = start + size
+                free[name] = start
             else:
-                margin = MARGIN if name in WITH_MARGIN else 0
-                start_of[name] = start_of["free"] + margin
-                start_of["free"] = start_of[name] + (size + ALIGN - 1) // ALIGN * ALIGN + margin
-            return work.tile(shape, dtype, name=name, align_bytes=ALIGN, offset=start_of[name])
+                margin = MARGIN if name in hosts else 0
+                start = free["fresh"] + margin
+                free["fresh"] = start + size + margin
+                if name in hosts:
+                    free[name, "first"] = start + max(SHARE, ALIGN)
+                    free[name] = start + max(SHARE, ALIGN)
+            end_of[name] = start + size
+            return work.tile(shape, dtype, name=name, align_bytes=ALIGN, offset=start)
 
         offsets = keep.tile([P, J // PER_COLUMN], U16, name="offsets")
         tab_plane = sb([P, T], U8, "tab_plane")
@@ -96,19 +105,38 @@ def tile_list_tiert_none_kernel(tc, tab_words, tab_scales, wt, x, wx_words, wx_s
         eye_plane = sb([P, KP], U8, "eye_plane")
         w_raw, w_bf, tab_raw, x_raw, x_bf = {}, {}, {}, {}, {}
         wq, wr, rest, back, words, xq = {}, {}, {}, {}, {}, {}
-        sums, passes_done = {}, {}
+        scales, sums, passes_done, results = {}, {}, {}, {}
 
         def listed(j0, j1):
             return offsets[:, j0 // PER_COLUMN : j1 // PER_COLUMN]
 
-        def load_w(a, u):
-            w_raw[a, u] = sb([P, PACK, HALF], F32, f"w_raw{a}{u}")
-            rows = wt[KP * a : KP * (a + 1), HALF * u : HALF * (u + 1)]
-            nc.sync.dma_start(w_raw[a, u][:], rows.rearrange("(p t) n -> p t n", t=PACK))
+        def columns(chunks):
+            return slice(CHUNK * chunks[0], CHUNK * (chunks[-1] + 1))
+
+        def load_w(a, chunks):
+            raw = sb([P, PACK, CHUNK * len(chunks)], F32, f"w_raw{a}{chunks[0]}")
+            nc.sync.dma_start(raw[:], wt[KP * a : KP * (a + 1), columns(chunks)].rearrange("(p t) n -> p t n", t=PACK))
+            for c in chunks:
+                w_raw[a, c] = (raw, CHUNK * (c - chunks[0]))
+
+        def raw_columns(a, chunks):
+            raw, first = w_raw[a, chunks[0]]
+            return raw[:, :, first : first + CHUNK * len(chunks)]
 
         def load_table(a):
             tab_raw[a] = sb([P, T], I32, f"tab_raw{a}")
             nc.sync.dma_start(tab_raw[a][:], tab_words[a].rearrange("p c t -> p (c t)").bitcast(I32))
+
+        def load_table_scales():
+            for q in range(4):
+                nc.sync.dma_start(tab_plane[32 * q : 32 * q + 8, :].bitcast(I32), tab_scales[:, 4 * q : 4 * q + 4, :].bitcast(I32))
+
+        def load_wx_scales():
+            for q in range(4):
+                nc.sync.dma_start(wx_plane[32 * q : 32 * q + 4, :].bitcast(I32), wx_scales[0, 4 * q : 4 * q + 4, :].bitcast(I32))
+
+        def load_wx_words():
+            nc.sync.dma_start(wx_codes[:].bitcast(I32), wx_words[0].bitcast(I32))
 
         def load_x(s):
             x_raw[s] = sb([P, PACK, QUARTER], F32, f"x_raw{s}")
@@ -122,10 +150,20 @@ def tile_list_tiert_none_kernel(tc, tab_words, tab_scales, wt, x, wx_words, wx_s
                     nc.vector.tensor_scalar(
                         out=eye[:, first : first + KP // 2], in0=ramp[:], scalar1=float(P + t - KP // 2 * h), scalar2=None, op0=mybir.AluOpType.is_equal
                     )
-            nc.vector.quantize_mx(out=eye_codes[:].bitcast(FP8X4), scales=eye_plane[:], in_=eye[:])
+            for h in range(2):
+                cols = slice(KP // 2 * h, KP // 2 * (h + 1))
+                nc.vector.quantize_mx(out=eye_codes[:, cols].bitcast(FP8X4), scales=eye_plane[:, cols], in_=eye[:, 2 * KP * h : 2 * KP * (h + 1)])
 
-        def gather_scales(tile, first, j0, j1):
-            nc.vector.tensor_copy(tile[:, j0 - first : j1 - first], tab_plane[:].indirect(listed(j0, j1)))
+        def gather_scales(j0, j1):
+            for first, last in ((0, 768), (768, 1024)):
+                if first <= j0 < last:
+                    if first not in scales:
+                        scales[first] = sb([P, last - first], U8, f"scales{first}")
+                    nc.vector.tensor_copy(scales[first][:, j0 - first : j1 - first], tab_plane[:].indirect(listed(j0, j1)))
+
+        def scales_of(a, j0, j1):
+            first = max(f for f in scales if f <= j0)
+            return scales[first][PACK * a : P, j0 - first : j1 - first]
 
         def gather_words(a, g):
             j0, j1 = SPANS[g]
@@ -139,9 +177,9 @@ def tile_list_tiert_none_kernel(tc, tab_words, tab_scales, wt, x, wx_words, wx_s
             codes, plane = operand
             nc.vector.quantize_mx(out=codes[:, cols].bitcast(FP8X4), scales=plane[:, cols], in_=grouped[:].rearrange("p c t -> p (c t)"))
 
-        def cast_w(a, u):
-            w_bf[a, u] = sb([P, HALF, PACK], BF16, f"w_bf{a}{u}")
-            nc.scalar.copy(out=woven(w_bf[a, u][:]), in_=by_rows(w_raw[a, u][:]))
+        def cast_w(a, chunks):
+            w_bf[a, chunks] = sb([P, CHUNK * len(chunks), PACK], BF16, f"w_bf{a}{chunks[0]}")
+            nc.scalar.copy(out=woven(w_bf[a, chunks][:]), in_=by_rows(raw_columns(a, chunks)))
 
         def cast_x(s):
             x_bf[s] = sb([P, QUARTER, PACK], BF16, f"x_bf{s}")
@@ -153,10 +191,11 @@ def tile_list_tiert_none_kernel(tc, tab_words, tab_scales, wt, x, wx_words, wx_s
                 cols = slice(CHUNK * i, CHUNK * (i + 1))
                 tier[a, c] = (codes[:, cols].bitcast(FP8X4), plane[:, cols])
 
-        def first_tier(a, u):
-            operand = mx_tiles(HALF, f"wq{a}{u}")
-            quantize(operand, slice(0, HALF), w_bf[a, u])
-            by_chunk(wq, a, (2 * u, 2 * u + 1), operand)
+        def first_tier(a, chunks):
+            width = CHUNK * len(chunks)
+            operand = mx_tiles(width, f"wq{a}{chunks[0]}")
+            quantize(operand, slice(0, width), w_bf[a, chunks])
+            by_chunk(wq, a, chunks, operand)
 
         def read_back(a, c):
             codes, plane = wq[a, c]
@@ -176,10 +215,9 @@ def tile_list_tiert_none_kernel(tc, tab_words, tab_scales, wt, x, wx_words, wx_s
             if (a, chunks) not in rest:
                 rest[a, chunks] = sb([P, CHUNK * len(chunks), PACK], BF16, f"rest{a}{chunks[0]}")
             place = CHUNK * chunks.index(c)
-            own = slice(CHUNK * (c % 2), CHUNK * (c % 2 + 1))
             nc.vector.tensor_tensor(
                 out=woven(rest[a, chunks][:, place : place + CHUNK, :]),
-                in0=by_rows(w_raw[a, c // 2][:, :, own]),
+                in0=by_rows(raw_columns(a, (c,))),
                 in1=by_rows(back[a, c][:]),
                 op=mybir.AluOpType.subtract,
             )
@@ -191,29 +229,36 @@ def tile_list_tiert_none_kernel(tc, tab_words, tab_scales, wt, x, wx_words, wx_s
             by_chunk(wr, a, chunks, operand)
 
         def quantize_x(s):
-            g = s // 2
+            g = max(s - 1, 0)
             j0, j1 = SPANS[g]
             if g not in xq:
                 xq[g] = mx_tiles(j1 - j0, f"xq{g}")
             quantize(xq[g], slice(QUARTER * s - j0, QUARTER * (s + 1) - j0), x_bf[s])
 
-        def last_quarter_of_x():
-            parts = []
-            for h in range(2):
-                part = sb([P, NARROW, PACK], BF16, f"x_last{h}")
-                nc.vector.tensor_copy(out=woven(part[:]), in_=by_rows(x_raw[3][:, :, NARROW * h : NARROW * (h + 1)]))
-                parts.append(part)
-            xq[2] = mx_tiles(QUARTER, "xq2")
-            for h in range(2):
-                quantize(xq[2], slice(NARROW * h, NARROW * (h + 1)), parts[h])
+        def cast_last_quarter():
+            x_bf[3] = sb([P, QUARTER, PACK], BF16, "x_bf3")
+            nc.vector.tensor_copy(out=woven(x_bf[3][:]), in_=by_rows(x_raw[3][:]))
+
+        def cast_last_part(h, on_vector):
+            x_bf[3, h] = sb([P, CHUNK, PACK], BF16, f"x_last{h}")
+            raw = by_rows(x_raw[3][:, :, CHUNK * h : CHUNK * (h + 1)])
+            if on_vector:
+                nc.vector.tensor_copy(out=woven(x_bf[3, h][:]), in_=raw)
+            else:
+                nc.scalar.copy(out=woven(x_bf[3, h][:]), in_=raw)
+
+        def quantize_last_part(h):
+            if 2 not in xq:
+                xq[2] = mx_tiles(QUARTER, "xq2")
+            quantize(xq[2], slice(CHUNK * h, CHUNK * (h + 1)), x_bf[3, h])
 
         def add_pass(c, g, j0, j1, lhsT, lhsT_scale, rhs, rhs_scale):
             if g == 0:
                 key, tag, first, count = (c, g), f"bank{c}", 0, 5
             elif g == 1:
-                key, tag, first, count = (c // 2, g), f"bank{4 + c // 2}", QUARTER * (c % 2), 12
+                key, tag, first, count = (c // 2, g), f"bank{4 + c // 2}", QUARTER * (c % 2), 10
             else:
-                key, tag, first, count = (c, g), LATE_BANKS[c], 0, 6
+                key, tag, first, count = (c, g), LATE_BANKS[c], 0, 5
             if key not in sums:
                 sums[key] = psum.tile([P, BANK], F32, name=f"sum{key[0]}{key[1]}", tag=tag)
                 passes_done[key] = 0
@@ -230,10 +275,9 @@ def tile_list_tiert_none_kernel(tc, tab_words, tab_scales, wt, x, wx_words, wx_s
 
         def table_passes(tier, a, chunks, g):
             j0, j1 = SPANS[g]
-            scales = scales_late[PACK * a : P, :] if g == 2 else scales_early[PACK * a : P, j0:j1]
             for c in chunks:
                 codes, plane = tier[a, c]
-                add_pass(c, g, 0, j1 - j0, codes, plane, words[a, g][:].bitcast(FP8X4), scales)
+                add_pass(c, g, 0, j1 - j0, codes, plane, words[a, g][:].bitcast(FP8X4), scales_of(a, j0, j1))
 
         def both_tiers(a, c, g):
             table_passes(wq, a, (c,), g)
@@ -242,16 +286,15 @@ def tile_list_tiert_none_kernel(tc, tab_words, tab_scales, wt, x, wx_words, wx_s
         def x_passes(chunks, g):
             codes, plane = xq[g]
             j0, j1 = SPANS[g]
-            width = BANK if g == 0 else NARROW
             for c in chunks:
                 stationary = wx_codes[:, 2 * CHUNK * c : 2 * CHUNK * (c + 1)].bitcast(FP4X4)
-                for j in range(0, j1 - j0, width):
-                    add_pass(c, g, j, j + width, stationary, wx_plane[:, CHUNK * c : CHUNK * (c + 1)], codes[:, j : j + width].bitcast(FP8X4), plane[:, j : j + width])
+                add_pass(c, g, 0, j1 - j0, stationary, wx_plane[:, CHUNK * c : CHUNK * (c + 1)], codes[:].bitcast(FP8X4), plane[:])
 
         def store(i, g, on_vector):
             j0, j1 = SPANS[g]
             width = QUARTER if g == 2 else BANK
             result = sb([P, width], F32, f"result{i}{g}")
+            results[i, g] = result
             if on_vector:
                 nc.vector.tensor_copy(out=result[:], in_=sums[i, g][:, 0:width])
             else:
@@ -263,59 +306,56 @@ def tile_list_tiert_none_kernel(tc, tab_words, tab_scales, wt, x, wx_words, wx_s
                 nc.sync.dma_start(out[CHUNK * i : CHUNK * (i + 1), j0:j1], result[:])
 
         nc.vector.memset(tab_plane[:].bitcast(I32), 0)
-        load_w(0, 0)
+        load_w(0, LOW)
         nc.sync.dma_start(offsets[:], offs)
-        for q in range(4):
-            nc.sync.dma_start(tab_plane[32 * q : 32 * q + 8, :].bitcast(I32), tab_scales[:, 4 * q : 4 * q + 4, :].bitcast(I32))
+        load_table_scales()
         nc.vector.memset(wx_plane[:].bitcast(I32), 0)
         make_identity_operand()
-        load_w(0, 1)
+        load_w(0, HIGH)
         load_table(0)
-        load_w(1, 0)
-        load_w(1, 1)
+        load_w(1, LOW)
+        load_w(1, HIGH)
         load_table(1)
-        for q in range(4):
-            nc.sync.dma_start(wx_plane[32 * q : 32 * q + 4, :].bitcast(I32), wx_scales[0, 4 * q : 4 * q + 4, :].bitcast(I32))
+        load_wx_scales()
         load_x(0)
-        nc.sync.dma_start(wx_codes[:].bitcast(I32), wx_words[0].bitcast(I32))
+        load_wx_words()
         for s in range(1, 4):
             load_x(s)
         for a in range(2):
-            for u in range(2):
-                cast_w(a, u)
+            cast_w(a, LOW)
+            cast_w(a, HIGH)
         for s in range(3):
             cast_x(s)
 
-        scales_early = sb([P, EARLY], U8, "scales_early")
-        gather_scales(scales_early, 0, 0, FIRST_SCALES)
-        first_tier(0, 0)
+        gather_scales(0, 256)
+        first_tier(0, LOW)
         read_back(0, 0)
         read_back(0, 1)
-        gather_scales(scales_early, 0, FIRST_SCALES, EARLY)
+        gather_scales(256, 768)
         subtract(0, 0, LOW)
-        first_tier(0, 1)
+        first_tier(0, HIGH)
         read_back(0, 2)
         subtract(0, 1, LOW)
         read_back(0, 3)
         gather_words(0, 0)
-        table_passes(wq, 0, range(4), 0)
+        table_passes(wq, 0, ALL, 0)
         second_tier(0, LOW)
         table_passes(wr, 0, LOW, 0)
         gather_words(0, 1)
-        table_passes(wq, 0, range(4), 1)
+        table_passes(wq, 0, ALL, 1)
         subtract(0, 2, HIGH)
         subtract(0, 3, HIGH)
-        first_tier(1, 0)
+        first_tier(1, LOW)
         read_back(1, 0)
         table_passes(wr, 0, LOW, 1)
         read_back(1, 1)
-        first_tier(1, 1)
+        first_tier(1, HIGH)
         second_tier(0, HIGH)
         for g in range(2):
             table_passes(wr, 0, HIGH, g)
 
         gather_words(1, 0)
-        table_passes(wq, 1, range(4), 0)
+        table_passes(wq, 1, ALL, 0)
         gather_words(1, 1)
         table_passes(wq, 1, LOW, 1)
         subtract(1, 0, LOW)
@@ -329,32 +369,35 @@ def tile_list_tiert_none_kernel(tc, tab_words, tab_scales, wt, x, wx_words, wx_s
             table_passes(wr, 1, LOW, g)
         subtract(1, 2, (2,))
         quantize_x(1)
-        x_passes(range(4), 0)
+        x_passes(ALL, 0)
         store(0, 0, False)
         store(1, 0, False)
+        second_tier(1, (2,))
+        table_passes(wr, 1, (2,), 0)
+        store(2, 0, False)
         subtract(1, 3, (3,))
-        for c in HIGH:
-            second_tier(1, (c,))
-        for c in HIGH:
-            table_passes(wr, 1, (c,), 0)
-            store(c, 0, False)
+        gather_scales(768, 1024)
+        second_tier(1, (3,))
+        table_passes(wr, 1, (3,), 0)
+        store(3, 0, False)
         table_passes(wr, 1, HIGH, 1)
-        quantize_x(2)
-        x_passes(range(4), 1)
-
-        scales_late = sb([P, J - EARLY], U8, "scales_late")
-        gather_scales(scales_late, EARLY, EARLY, J)
         gather_words(0, 2)
+        quantize_x(2)
+        x_passes(ALL, 1)
+        store(0, 1, False)
+        store(1, 1, False)
+
         for c in LOW:
             both_tiers(0, c, 2)
         gather_words(1, 2)
-        store(0, 1, False)
-        store(1, 1, False)
         for c in LOW:
             both_tiers(1, c, 2)
         for a in range(2):
             both_tiers(a, 2, 2)
-        last_quarter_of_x()
+        cast_last_part(0, True)
+        cast_last_part(1, True)
+        quantize_last_part(0)
+        quantize_last_part(1)
         for c in range(3):
             x_passes((c,), 2)
             store(c, 2, c % 2 == 1)

@@ -28,15 +28,15 @@ PER_COLUMN = 16
 SPANS = ((0, 512), (512, 768), (768, 1024))
 LATE_BANKS = ("back0", "back1", "bank0", "bank1")
 ALIGN = 64
+STRIPE = 256
 SHARE = 64
 MARGIN = 2048
 
 PLACED_ON = {
     "scales0": "eye",
     "wq00_codes": "eye",
-    "w_bf02": "w_bf00",
-    "words00": "w_bf02",
-    "words01": "w_raw00",
+    "words00": "w_bf00",
+    "words01": "w_bf00",
     "words10": "w_bf12",
     "words11": "w_bf12",
     "rest12": "x_raw0",
@@ -51,6 +51,7 @@ PLACED_ON = {
     "x_last0": "x_bf2",
     "x_last1": "x_raw2",
 }
+SAME_BYTES = {"w_bf02": "w_bf00"}
 
 
 def woven(ap):
@@ -76,18 +77,26 @@ def tile_list_tiert_none_kernel(tc, tab_words, tab_scales, wt, x, wx_words, wx_s
             for extent in shape[1:]:
                 size = size * extent
             size = (size + ALIGN - 1) // ALIGN * ALIGN
-            if name in PLACED_ON:
+            phase = ALIGN if name.startswith("words") or (name.startswith("xq") and name[-5:] == "codes") else 0
+            if name in SAME_BYTES:
+                start = end_of[SAME_BYTES[name]] - size
+            elif name in PLACED_ON:
                 spent = PLACED_ON[name]
-                start = free[spent]
+                start = free[spent] + (phase - free[spent]) % STRIPE
                 if (spent, "first") in free:
                     start = free.pop((spent, "first")) - size
-                else:
-                    assert start < end_of[spent] and start + size <= end_of[spent] + (0 if spent in PLACED_ON else MARGIN), name
+                    start = start + (phase - start) % STRIPE
                     free[spent] = start + size
+                else:
+                    assert start < end_of[spent] and start + size <= end_of[spent] + (STRIPE if spent in PLACED_ON else MARGIN), name
+                    free[spent] = start + size
+                if name in hosts:
+                    free[spent] = free[spent] + STRIPE
                 free[name] = start
             else:
                 margin = MARGIN if name in hosts else 0
                 start = free["fresh"] + margin
+                start = start + (phase - start) % STRIPE
                 free["fresh"] = start + size + margin
                 if name in hosts:
                     free[name, "first"] = start + max(SHARE, ALIGN)

@@ -102,7 +102,7 @@ def tile_list_tiert_none_kernel(tc, tab_words, tab_scales, wt, x, wx_words, wx_s
                     free[name, "first"] = start + max(SHARE, ALIGN)
                     free[name] = start + max(SHARE, ALIGN)
             end_of[name] = start + size
-            return work.tile(shape, dtype, name=name, align_bytes=ALIGN, offset=start)
+            return work.tile(shape, dtype, name=name, align_bytes=ALIGN if start % STRIPE else STRIPE, offset=start)
 
         offsets = keep.tile([P, J // PER_COLUMN], U16, name="offsets")
         tab_plane = sb([P, T], U8, "tab_plane")

@@ -16,42 +16,42 @@ FP4X4 = mybir.dt.float4_e2m1fn_x4
 BYTES_OF = {F32: 4, BF16: 2, I32: 4, U32: 4, U8: 1}
 
 P = 128
+QUADRANT = 32
 PACK = 4
 KP = P * PACK
 CHUNK = 128
-HALF = 2 * CHUNK
-LOW, HIGH = (0, 1), (2, 3)
-ALL = (0, 1, 2, 3)
+LOW, HIGH, ALL = (0, 1), (2, 3), (0, 1, 2, 3)
 QUARTER = J // 4
 BANK = 512
 PER_COLUMN = 16
-SPANS = ((0, 512), (512, 768), (768, 1024))
-LATE_BANKS = ("back0", "back1", "bank0", "bank1")
-ALIGN = 64
+SPANS = {"A": (0, 512), "B": (512, 768), "C": (768, 1024)}
 STRIPE = 256
-SHARE = 64
-MARGIN = 2048
+SHIFT = 64
+ROOM = 2048
 
 PLACED_ON = {
     "scales0": "eye",
     "wq00_codes": "eye",
-    "words00": "w_bf00",
-    "words01": "w_bf00",
-    "words10": "w_bf12",
-    "words11": "w_bf12",
-    "rest12": "x_raw0",
-    "wr10_plane": "x_raw0",
+    "words0A": "w_bf00",
+    "words0B": "w_bf00",
+    "words1A": "w_bf12",
     "wr12_plane": "x_raw1",
     "rest13": "x_raw1",
-    "result00": "x_raw2",
-    "result10": "x_raw2",
+    "result0A": "x_raw2",
+    "result1A": "x_raw2",
     "scales768": "rest12",
-    "words02": "rest13",
-    "words12": "x_bf2",
-    "x_last0": "x_bf2",
-    "x_last1": "x_raw2",
+    "words0C": "x_raw2",
+    "words1C": "x_bf512",
+    "x_bf768": "x_bf512",
+    "x_bf896": "x_raw2",
+    "rest12": "x_raw0",
 }
-SAME_BYTES = {"w_bf02": "w_bf00"}
+SAME_BYTES = {"w_bf02": "w_bf00", "words1B": "words0B"}
+SUMS = {
+    "A": [(f"sumA{c}", f"bank{c}", 0, 1) for c in ALL],
+    "B": [(f"sumB{c // 2}", f"bank{4 + c // 2}", QUARTER * (c % 2), 2) for c in ALL],
+    "C": [(f"sumC{c}", bank, 0, 1) for c, bank in enumerate(("back0", "back1", "bank0", "bank1"))],
+}
 
 
 def woven(ap):
@@ -62,47 +62,47 @@ def by_rows(ap):
     return ap.rearrange("p t (c i) -> p c t i", i=2)
 
 
+def round_up(value, step):
+    return (value + step - 1) // step * step
+
+
 def tile_list_tiert_none_kernel(tc, tab_words, tab_scales, wt, x, wx_words, wx_scales, offs, out):
     nc = tc.nc
     with ExitStack() as ctx:
         keep = ctx.enter_context(tc.tile_pool(name="keep", bufs=1))
         work = ctx.enter_context(tc.tile_pool(name="work", bufs=1))
         psum = ctx.enter_context(tc.psum_pool(name="psum", bufs=1))
-        hosts = set(PLACED_ON.values())
-        free = {"fresh": 0}
-        end_of = {}
+        spent = set(PLACED_ON.values())
+        extent = {}
+        cursor = {"fresh": 0}
+        placed = {}
 
-        def sb(shape, dtype, name):
+        def sb(shape, dtype, name, moving=False):
             size = BYTES_OF[dtype]
-            for extent in shape[1:]:
-                size = size * extent
-            size = (size + ALIGN - 1) // ALIGN * ALIGN
-            phase = ALIGN if name.startswith("words") or (name.startswith("xq") and name[-5:] == "codes") else 0
+            for count in shape[1:]:
+                size = size * count
+            shift = SHIFT if moving else 0
+            length = round_up(size + shift, STRIPE)
+            host = PLACED_ON.get(name)
             if name in SAME_BYTES:
-                start = end_of[SAME_BYTES[name]] - size
-            elif name in PLACED_ON:
-                spent = PLACED_ON[name]
-                start = free[spent] + (phase - free[spent]) % STRIPE
-                if (spent, "first") in free:
-                    start = free.pop((spent, "first")) - size
-                    start = start + (phase - start) % STRIPE
-                    free[spent] = start + size
-                else:
-                    assert start < end_of[spent] and start + size <= end_of[spent] + (STRIPE if spent in PLACED_ON else MARGIN), name
-                    free[spent] = start + size
-                if name in hosts:
-                    free[spent] = free[spent] + STRIPE
-                free[name] = start
+                start = extent[SAME_BYTES[name]][0]
+            elif host is None:
+                room = ROOM if name in spent else 0
+                start = cursor["fresh"] + room
+                cursor["fresh"] = start + length + room
             else:
-                margin = MARGIN if name in hosts else 0
-                start = free["fresh"] + margin
-                start = start + (phase - start) % STRIPE
-                free["fresh"] = start + size + margin
-                if name in hosts:
-                    free[name, "first"] = start + max(SHARE, ALIGN)
-                    free[name] = start + max(SHARE, ALIGN)
-            end_of[name] = start + size
-            return work.tile(shape, dtype, name=name, align_bytes=ALIGN if start % STRIPE else STRIPE, offset=start)
+                begin, end = extent[host]
+                placed[host] = placed.get(host, 0) + 1
+                if host not in PLACED_ON and placed[host] == 1:
+                    start = begin + STRIPE - length
+                elif host not in PLACED_ON and placed[host] == 2:
+                    start = end - STRIPE
+                else:
+                    start = cursor.get(host, begin if host in PLACED_ON else begin + STRIPE)
+                    cursor[host] = start + length
+                    assert start + shift < end, name
+            extent[name] = (start, start + length)
+            return work.tile(shape, dtype, name=name, align_bytes=SHIFT if moving else STRIPE, offset=start + shift)
 
         offsets = keep.tile([P, J // PER_COLUMN], U16, name="offsets")
         tab_plane = sb([P, T], U8, "tab_plane")
@@ -113,36 +113,35 @@ def tile_list_tiert_none_kernel(tc, tab_words, tab_scales, wt, x, wx_words, wx_s
         eye_codes = sb([P, KP], U32, "eye_codes")
         eye_plane = sb([P, KP], U8, "eye_plane")
         w_raw, w_bf, tab_raw, x_raw, x_bf = {}, {}, {}, {}, {}
-        wq, wr, rest, back, words, xq = {}, {}, {}, {}, {}, {}
-        scales, sums, passes_done, results = {}, {}, {}, {}
+        first, second, rest, back, words, scales, xq = {}, {}, {}, {}, {}, {}, {}
+        sums, passes_left, results = {}, {}, {}
 
         def listed(j0, j1):
             return offsets[:, j0 // PER_COLUMN : j1 // PER_COLUMN]
 
-        def columns(chunks):
-            return slice(CHUNK * chunks[0], CHUNK * (chunks[-1] + 1))
-
         def load_w(a, chunks):
             raw = sb([P, PACK, CHUNK * len(chunks)], F32, f"w_raw{a}{chunks[0]}")
-            nc.sync.dma_start(raw[:], wt[KP * a : KP * (a + 1), columns(chunks)].rearrange("(p t) n -> p t n", t=PACK))
+            cols = slice(CHUNK * chunks[0], CHUNK * (chunks[-1] + 1))
+            nc.sync.dma_start(raw[:], wt[KP * a : KP * (a + 1), cols].rearrange("(p t) n -> p t n", t=PACK))
             for c in chunks:
                 w_raw[a, c] = (raw, CHUNK * (c - chunks[0]))
 
         def raw_columns(a, chunks):
-            raw, first = w_raw[a, chunks[0]]
-            return raw[:, :, first : first + CHUNK * len(chunks)]
+            raw, at = w_raw[a, chunks[0]]
+            return raw[:, :, at : at + CHUNK * len(chunks)]
 
         def load_table(a):
             tab_raw[a] = sb([P, T], I32, f"tab_raw{a}")
             nc.sync.dma_start(tab_raw[a][:], tab_words[a].rearrange("p c t -> p (c t)").bitcast(I32))
 
-        def load_table_scales():
-            for q in range(4):
-                nc.sync.dma_start(tab_plane[32 * q : 32 * q + 8, :].bitcast(I32), tab_scales[:, 4 * q : 4 * q + 4, :].bitcast(I32))
+        def load_table_scales(queue, q):
+            rows = tab_plane[QUADRANT * q : QUADRANT * q + 2 * PACK, :]
+            queue.dma_start(rows.bitcast(I32), tab_scales[:, PACK * q : PACK * (q + 1), :].bitcast(I32))
 
         def load_wx_scales():
             for q in range(4):
-                nc.sync.dma_start(wx_plane[32 * q : 32 * q + 4, :].bitcast(I32), wx_scales[0, 4 * q : 4 * q + 4, :].bitcast(I32))
+                rows = wx_plane[QUADRANT * q : QUADRANT * q + PACK, :]
+                nc.sync.dma_start(rows.bitcast(I32), wx_scales[0, PACK * q : PACK * (q + 1), :].bitcast(I32))
 
         def load_wx_words():
             nc.sync.dma_start(wx_codes[:].bitcast(I32), wx_words[0].bitcast(I32))
@@ -151,175 +150,137 @@ def tile_list_tiert_none_kernel(tc, tab_words, tab_scales, wt, x, wx_words, wx_s
             x_raw[s] = sb([P, PACK, QUARTER], F32, f"x_raw{s}")
             nc.sync.dma_start(x_raw[s][:], x[:, QUARTER * s : QUARTER * (s + 1)].rearrange("(p t) j -> p t j", t=PACK))
 
-        def make_identity_operand():
+        def make_ramp():
             nc.gpsimd.iota(ramp[:], pattern=[[1, KP // 2]], base=P, channel_multiplier=-PACK, allow_small_or_imprecise_dtypes=True)
+
+        def make_identity():
             for t in range(PACK):
                 for h in range(2):
-                    first = KP * t + KP // 2 * h
+                    at = KP * t + KP // 2 * h
                     nc.vector.tensor_scalar(
-                        out=eye[:, first : first + KP // 2], in0=ramp[:], scalar1=float(P + t - KP // 2 * h), scalar2=None, op0=mybir.AluOpType.is_equal
+                        out=eye[:, at : at + KP // 2], in0=ramp[:], scalar1=float(P + t - KP // 2 * h), scalar2=None, op0=mybir.AluOpType.is_equal
                     )
             for h in range(2):
                 cols = slice(KP // 2 * h, KP // 2 * (h + 1))
                 nc.vector.quantize_mx(out=eye_codes[:, cols].bitcast(FP8X4), scales=eye_plane[:, cols], in_=eye[:, 2 * KP * h : 2 * KP * (h + 1)])
 
         def gather_scales(j0, j1):
-            for first, last in ((0, 768), (768, 1024)):
-                if first <= j0 < last:
-                    if first not in scales:
-                        scales[first] = sb([P, last - first], U8, f"scales{first}")
-                    nc.vector.tensor_copy(scales[first][:, j0 - first : j1 - first], tab_plane[:].indirect(listed(j0, j1)))
+            base = 0 if j0 < SPANS["C"][0] else SPANS["C"][0]
+            if base not in scales:
+                scales[base] = sb([P, SPANS["C"][0] if base == 0 else QUARTER], U8, f"scales{base}")
+            nc.vector.tensor_copy(scales[base][:, j0 - base : j1 - base], tab_plane[:].indirect(listed(j0, j1)))
 
-        def scales_of(a, j0, j1):
-            first = max(f for f in scales if f <= j0)
-            return scales[first][PACK * a : P, j0 - first : j1 - first]
+        def gather_words(a, span):
+            j0, j1 = SPANS[span]
+            words[a, span] = sb([P, j1 - j0], U32, f"words{a}{span}", moving=True)
+            nc.vector.tensor_copy(words[a, span][:], tab_raw[a][:].bitcast(U32).indirect(listed(j0, j1)))
 
-        def gather_words(a, g):
-            j0, j1 = SPANS[g]
-            words[a, g] = sb([P, j1 - j0], U32, f"words{a}{g}")
-            nc.vector.tensor_copy(words[a, g][:], tab_raw[a][:].bitcast(U32).indirect(listed(j0, j1)))
+        def quantize(codes, plane, grouped):
+            nc.vector.quantize_mx(out=codes.bitcast(FP8X4), scales=plane, in_=grouped[:].rearrange("p c t -> p (c t)"))
 
-        def mx_tiles(width, name):
-            return sb([P, width], U32, name + "_codes"), sb([P, width], U8, name + "_plane")
-
-        def quantize(operand, cols, grouped):
-            codes, plane = operand
-            nc.vector.quantize_mx(out=codes[:, cols].bitcast(FP8X4), scales=plane[:, cols], in_=grouped[:].rearrange("p c t -> p (c t)"))
+        def quantize_weights(tier, name, a, chunks, grouped):
+            codes = sb([P, CHUNK * len(chunks)], U32, f"{name}{a}{chunks[0]}_codes")
+            plane = sb([P, CHUNK * len(chunks)], U8, f"{name}{a}{chunks[0]}_plane")
+            quantize(codes[:], plane[:], grouped)
+            for i, c in enumerate(chunks):
+                cols = slice(CHUNK * i, CHUNK * (i + 1))
+                tier[a, c] = (codes[:, cols].bitcast(FP8X4), plane[:, cols])
 
         def cast_w(a, chunks):
             w_bf[a, chunks] = sb([P, CHUNK * len(chunks), PACK], BF16, f"w_bf{a}{chunks[0]}")
             nc.scalar.copy(out=woven(w_bf[a, chunks][:]), in_=by_rows(raw_columns(a, chunks)))
 
-        def cast_x(s):
-            x_bf[s] = sb([P, QUARTER, PACK], BF16, f"x_bf{s}")
-            nc.scalar.copy(out=woven(x_bf[s][:]), in_=by_rows(x_raw[s][:]))
-
-        def by_chunk(tier, a, chunks, operand):
-            codes, plane = operand
-            for i, c in enumerate(chunks):
-                cols = slice(CHUNK * i, CHUNK * (i + 1))
-                tier[a, c] = (codes[:, cols].bitcast(FP8X4), plane[:, cols])
-
         def first_tier(a, chunks):
-            width = CHUNK * len(chunks)
-            operand = mx_tiles(width, f"wq{a}{chunks[0]}")
-            quantize(operand, slice(0, width), w_bf[a, chunks])
-            by_chunk(wq, a, chunks, operand)
+            quantize_weights(first, "wq", a, chunks, w_bf[a, chunks])
 
         def read_back(a, c):
-            codes, plane = wq[a, c]
+            codes, plane = first[a, c]
             back[a, c] = psum.tile([P, PACK, CHUNK], F32, name="back", tag=f"back{c % 2}")
             for t in range(PACK):
+                cols = slice(P * t, P * (t + 1))
                 nc.tensor.matmul_mx(
-                    out=back[a, c][:, t, :],
-                    lhsT=eye_codes[:, P * t : P * (t + 1)].bitcast(FP8X4),
-                    lhsT_scale=eye_plane[:, P * t : P * (t + 1)],
-                    rhs=codes,
-                    rhs_scale=plane,
-                    start=True,
-                    stop=True,
+                    out=back[a, c][:, t, :], lhsT=eye_codes[:, cols].bitcast(FP8X4), lhsT_scale=eye_plane[:, cols], rhs=codes, rhs_scale=plane, start=True, stop=True
                 )
 
         def subtract(a, c, chunks):
             if (a, chunks) not in rest:
                 rest[a, chunks] = sb([P, CHUNK * len(chunks), PACK], BF16, f"rest{a}{chunks[0]}")
-            place = CHUNK * chunks.index(c)
+            at = CHUNK * chunks.index(c)
             nc.vector.tensor_tensor(
-                out=woven(rest[a, chunks][:, place : place + CHUNK, :]),
-                in0=by_rows(raw_columns(a, (c,))),
-                in1=by_rows(back[a, c][:]),
-                op=mybir.AluOpType.subtract,
+                out=woven(rest[a, chunks][:, at : at + CHUNK, :]), in0=by_rows(raw_columns(a, (c,))), in1=by_rows(back[a, c][:]), op=mybir.AluOpType.subtract
             )
 
         def second_tier(a, chunks):
-            width = CHUNK * len(chunks)
-            operand = mx_tiles(width, f"wr{a}{chunks[0]}")
-            quantize(operand, slice(0, width), rest[a, chunks])
-            by_chunk(wr, a, chunks, operand)
+            quantize_weights(second, "wr", a, chunks, rest[a, chunks])
 
-        def quantize_x(s):
-            g = max(s - 1, 0)
-            j0, j1 = SPANS[g]
-            if g not in xq:
-                xq[g] = mx_tiles(j1 - j0, f"xq{g}")
-            quantize(xq[g], slice(QUARTER * s - j0, QUARTER * (s + 1) - j0), x_bf[s])
+        def cast_x(j0, j1, engine_copy):
+            x_bf[j0] = sb([P, j1 - j0, PACK], BF16, f"x_bf{j0}")
+            s = j0 // QUARTER
+            engine_copy(out=woven(x_bf[j0][:]), in_=by_rows(x_raw[s][:, :, j0 - QUARTER * s : j1 - QUARTER * s]))
 
-        def cast_last_quarter():
-            x_bf[3] = sb([P, QUARTER, PACK], BF16, "x_bf3")
-            nc.vector.tensor_copy(out=woven(x_bf[3][:]), in_=by_rows(x_raw[3][:]))
+        def quantize_x(j0, j1):
+            s = j0 // QUARTER
+            if s not in xq:
+                xq[s] = (sb([P, QUARTER], U32, f"xq{s}_codes", moving=True), sb([P, QUARTER], U8, f"xq{s}_plane"))
+            codes, plane = xq[s]
+            cols = slice(j0 - QUARTER * s, j1 - QUARTER * s)
+            quantize(codes[:, cols], plane[:, cols], x_bf[j0])
 
-        def cast_last_part(h, on_vector):
-            x_bf[3, h] = sb([P, CHUNK, PACK], BF16, f"x_last{h}")
-            raw = by_rows(x_raw[3][:, :, CHUNK * h : CHUNK * (h + 1)])
-            if on_vector:
-                nc.vector.tensor_copy(out=woven(x_bf[3, h][:]), in_=raw)
-            else:
-                nc.scalar.copy(out=woven(x_bf[3, h][:]), in_=raw)
-
-        def quantize_last_part(h):
-            if 2 not in xq:
-                xq[2] = mx_tiles(QUARTER, "xq2")
-            quantize(xq[2], slice(CHUNK * h, CHUNK * (h + 1)), x_bf[3, h])
-
-        def add_pass(c, g, j0, j1, lhsT, lhsT_scale, rhs, rhs_scale):
-            if g == 0:
-                key, tag, first, count = (c, g), f"bank{c}", 0, 5
-            elif g == 1:
-                key, tag, first, count = (c // 2, g), f"bank{4 + c // 2}", QUARTER * (c % 2), 10
-            else:
-                key, tag, first, count = (c, g), LATE_BANKS[c], 0, 5
-            if key not in sums:
-                sums[key] = psum.tile([P, BANK], F32, name=f"sum{key[0]}{key[1]}", tag=tag)
-                passes_done[key] = 0
+        def add_pass(c, span, j0, j1, lhsT, lhsT_scale, rhs, rhs_scale):
+            name, bank, at, chunks_in_bank = SUMS[span][c]
+            base, end = SPANS[span]
+            count = (4 + (end - base) // QUARTER) * chunks_in_bank
+            if name not in sums:
+                sums[name] = psum.tile([P, BANK], F32, name=name, tag=bank)
+                passes_left[name] = count
             nc.tensor.matmul_mx(
-                out=sums[key][:, first + j0 : first + j1],
+                out=sums[name][:, at + j0 - base : at + j1 - base],
                 lhsT=lhsT,
                 lhsT_scale=lhsT_scale,
                 rhs=rhs,
                 rhs_scale=rhs_scale,
-                start=(passes_done[key] == 0),
-                stop=(passes_done[key] == count - 1),
+                start=(passes_left[name] == count),
+                stop=(passes_left[name] == 1),
             )
-            passes_done[key] = passes_done[key] + 1
+            passes_left[name] = passes_left[name] - 1
 
-        def table_passes(tier, a, chunks, g):
-            j0, j1 = SPANS[g]
+        def table_passes(tier, a, chunks, span):
+            j0, j1 = SPANS[span]
+            base = max(b for b in scales if b <= j0)
             for c in chunks:
                 codes, plane = tier[a, c]
-                add_pass(c, g, 0, j1 - j0, codes, plane, words[a, g][:].bitcast(FP8X4), scales_of(a, j0, j1))
+                add_pass(c, span, j0, j1, codes, plane, words[a, span][:].bitcast(FP8X4), scales[base][PACK * a : P, j0 - base : j1 - base])
 
-        def both_tiers(a, c, g):
-            table_passes(wq, a, (c,), g)
-            table_passes(wr, a, (c,), g)
+        def both_tiers(a, c, span):
+            table_passes(first, a, (c,), span)
+            table_passes(second, a, (c,), span)
 
-        def x_passes(chunks, g):
-            codes, plane = xq[g]
-            j0, j1 = SPANS[g]
+        def x_passes(chunks, s):
+            codes, plane = xq[s]
             for c in chunks:
                 stationary = wx_codes[:, 2 * CHUNK * c : 2 * CHUNK * (c + 1)].bitcast(FP4X4)
-                add_pass(c, g, 0, j1 - j0, stationary, wx_plane[:, CHUNK * c : CHUNK * (c + 1)], codes[:].bitcast(FP8X4), plane[:])
+                scale = wx_plane[:, CHUNK * c : CHUNK * (c + 1)]
+                add_pass(c, "AABC"[s], QUARTER * s, QUARTER * (s + 1), stationary, scale, codes[:].bitcast(FP8X4), plane[:])
 
-        def store(i, g, on_vector):
-            j0, j1 = SPANS[g]
-            width = QUARTER if g == 2 else BANK
-            result = sb([P, width], F32, f"result{i}{g}")
-            results[i, g] = result
-            if on_vector:
-                nc.vector.tensor_copy(out=result[:], in_=sums[i, g][:, 0:width])
-            else:
-                nc.scalar.copy(out=result[:], in_=sums[i, g][:, 0:width])
-            if g == 1:
-                rows = out[HALF * i : HALF * (i + 1), j0:j1].rearrange("(c p) j -> p c j", p=P)
-                nc.sync.dma_start(rows, result[:].rearrange("p (c j) -> p c j", c=2))
-            else:
-                nc.sync.dma_start(out[CHUNK * i : CHUNK * (i + 1), j0:j1], result[:])
+        def store(c, span, engine_copy):
+            name, bank, at, count = SUMS[span][c]
+            j0, j1 = SPANS[span]
+            result = sb([P, count, j1 - j0], F32, f"result{c}{span}")
+            results[c, span] = result
+            engine_copy(out=result[:].rearrange("p c j -> p (c j)"), in_=sums[name][:, 0 : count * (j1 - j0)])
+            rows = out[CHUNK * c : CHUNK * (c + count), j0:j1].rearrange("(c p) j -> p c j", p=P)
+            nc.sync.dma_start(rows, result[:])
+
+        on_scalar, on_vector = nc.scalar.copy, nc.vector.tensor_copy
 
         nc.vector.memset(tab_plane[:].bitcast(I32), 0)
         load_w(0, LOW)
         nc.sync.dma_start(offsets[:], offs)
-        load_table_scales()
+        for q in range(4):
+            load_table_scales(nc.sync, q)
         nc.vector.memset(wx_plane[:].bitcast(I32), 0)
-        make_identity_operand()
+        make_ramp()
+        make_identity()
         load_w(0, HIGH)
         load_table(0)
         load_w(1, LOW)
@@ -334,7 +295,7 @@ def tile_list_tiert_none_kernel(tc, tab_words, tab_scales, wt, x, wx_words, wx_s
             cast_w(a, LOW)
             cast_w(a, HIGH)
         for s in range(3):
-            cast_x(s)
+            cast_x(QUARTER * s, QUARTER * (s + 1), on_scalar)
 
         gather_scales(0, 256)
         first_tier(0, LOW)
@@ -346,71 +307,73 @@ def tile_list_tiert_none_kernel(tc, tab_words, tab_scales, wt, x, wx_words, wx_s
         read_back(0, 2)
         subtract(0, 1, LOW)
         read_back(0, 3)
-        gather_words(0, 0)
-        table_passes(wq, 0, ALL, 0)
+        gather_words(0, "B")
+        table_passes(first, 0, ALL, "B")
         second_tier(0, LOW)
-        table_passes(wr, 0, LOW, 0)
-        gather_words(0, 1)
-        table_passes(wq, 0, ALL, 1)
+        table_passes(second, 0, LOW, "B")
+        gather_words(0, "A")
+        table_passes(first, 0, ALL, "A")
         subtract(0, 2, HIGH)
         subtract(0, 3, HIGH)
         first_tier(1, LOW)
+        table_passes(second, 0, LOW, "A")
         read_back(1, 0)
-        table_passes(wr, 0, LOW, 1)
         read_back(1, 1)
         first_tier(1, HIGH)
         second_tier(0, HIGH)
-        for g in range(2):
-            table_passes(wr, 0, HIGH, g)
+        for span in "AB":
+            table_passes(second, 0, HIGH, span)
 
-        gather_words(1, 0)
-        table_passes(wq, 1, ALL, 0)
-        gather_words(1, 1)
-        table_passes(wq, 1, LOW, 1)
+        gather_words(1, "A")
+        table_passes(first, 1, LOW, "A")
         subtract(1, 0, LOW)
+        table_passes(first, 1, (2,), "A")
         read_back(1, 2)
-        table_passes(wq, 1, HIGH, 1)
+        table_passes(first, 1, (3,), "A")
         subtract(1, 1, LOW)
         read_back(1, 3)
-        quantize_x(0)
+        gather_words(1, "B")
+        table_passes(first, 1, ALL, "B")
         second_tier(1, LOW)
-        for g in range(2):
-            table_passes(wr, 1, LOW, g)
-        subtract(1, 2, (2,))
-        quantize_x(1)
+        for span in "AB":
+            table_passes(second, 1, LOW, span)
+        quantize_x(0, 256)
         x_passes(ALL, 0)
-        store(0, 0, False)
-        store(1, 0, False)
+        subtract(1, 2, (2,))
+        quantize_x(256, 512)
+        x_passes(ALL, 1)
+        store(0, "A", on_scalar)
+        store(1, "A", on_scalar)
         second_tier(1, (2,))
-        table_passes(wr, 1, (2,), 0)
-        store(2, 0, False)
+        table_passes(second, 1, (2,), "A")
+        store(2, "A", on_scalar)
         subtract(1, 3, (3,))
         gather_scales(768, 1024)
         second_tier(1, (3,))
-        table_passes(wr, 1, (3,), 0)
-        store(3, 0, False)
-        table_passes(wr, 1, HIGH, 1)
-        gather_words(0, 2)
-        quantize_x(2)
-        x_passes(ALL, 1)
-        store(0, 1, False)
-        store(1, 1, False)
+        table_passes(second, 1, (3,), "A")
+        store(3, "A", on_scalar)
+        table_passes(second, 1, HIGH, "B")
+        quantize_x(512, 768)
+        x_passes(ALL, 2)
+        store(0, "B", on_scalar)
+        store(2, "B", on_scalar)
+        gather_words(0, "C")
 
         for c in LOW:
-            both_tiers(0, c, 2)
-        gather_words(1, 2)
+            both_tiers(0, c, "C")
+        gather_words(1, "C")
         for c in LOW:
-            both_tiers(1, c, 2)
+            both_tiers(1, c, "C")
         for a in range(2):
-            both_tiers(a, 2, 2)
-        cast_last_part(0, True)
-        cast_last_part(1, True)
-        quantize_last_part(0)
-        quantize_last_part(1)
+            both_tiers(a, 2, "C")
+        cast_x(768, 896, on_vector)
+        cast_x(896, 1024, on_vector)
+        quantize_x(768, 896)
+        quantize_x(896, 1024)
         for c in range(3):
-            x_passes((c,), 2)
-            store(c, 2, c % 2 == 1)
+            x_passes((c,), 3)
+            store(c, "C", on_vector if c == 1 else on_scalar)
         for a in range(2):
-            both_tiers(a, 3, 2)
-        x_passes((3,), 2)
-        store(3, 2, True)
+            both_tiers(a, 3, "C")
+        x_passes((3,), 3)
+        store(3, "C", on_vector)

from contextlib import ExitStack

import concourse.mybir as mybir

K, L, N, T, J = 1024, 512, 512, 2048, 1024
FLOPS = 3221225472

F32 = mybir.dt.float32
BF16 = mybir.dt.bfloat16
I32 = mybir.dt.int32
U32 = mybir.dt.uint32
U16 = mybir.dt.uint16
U8 = mybir.dt.uint8
FP8X4 = mybir.dt.float8_e4m3fn_x4
FP4X4 = mybir.dt.float4_e2m1fn_x4
BYTES_OF = {F32: 4, BF16: 2, I32: 4, U32: 4, U8: 1}

P = 128
QUADRANT = 32
PACK = 4
KP = P * PACK
CHUNK = 128
LOW, HIGH, ALL = (0, 1), (2, 3), (0, 1, 2, 3)
QUARTER = J // 4
BANK = 512
PER_COLUMN = 16
SPANS = {"A": (0, 512), "B": (512, 768), "C": (768, 1024)}
STRIPE = 256
SHIFT = 64
ROOM = 2048

PLACED_ON = {
    "scales0": "eye",
    "wq00_codes": "eye",
    "words0A": "w_bf00",
    "words0B": "w_bf00",
    "words1A": "w_bf12",
    "wr12_plane": "x_raw1",
    "rest13": "x_raw1",
    "result0A": "x_raw2",
    "result1A": "x_raw2",
    "scales768": "rest12",
    "words0C": "x_raw2",
    "words1C": "x_bf512",
    "x_bf768": "x_bf512",
    "x_bf896": "x_raw2",
    "rest12": "x_raw0",
}
SAME_BYTES = {"w_bf02": "w_bf00", "words1B": "words0B"}
SUMS = {
    "A": [(f"sumA{c}", f"bank{c}", 0, 1) for c in ALL],
    "B": [(f"sumB{c // 2}", f"bank{4 + c // 2}", QUARTER * (c % 2), 2) for c in ALL],
    "C": [(f"sumC{c}", bank, 0, 1) for c, bank in enumerate(("back0", "back1", "bank0", "bank1"))],
}


def woven(ap):
    return ap.rearrange("p (c i) t -> p c t i", i=2)


def by_rows(ap):
    return ap.rearrange("p t (c i) -> p c t i", i=2)


def round_up(value, step):
    return (value + step - 1) // step * step


def tile_list_tiert_none_kernel(tc, tab_words, tab_scales, wt, x, wx_words, wx_scales, offs, out):
    nc = tc.nc
    with ExitStack() as ctx:
        keep = ctx.enter_context(tc.tile_pool(name="keep", bufs=1))
        work = ctx.enter_context(tc.tile_pool(name="work", bufs=1))
        psum = ctx.enter_context(tc.psum_pool(name="psum", bufs=1))
        spent = set(PLACED_ON.values())
        extent = {}
        cursor = {"fresh": 0}
        placed = {}

        def sb(shape, dtype, name, moving=False):
            size = BYTES_OF[dtype]
            for count in shape[1:]:
                size = size * count
            shift = SHIFT if moving else 0
            length = round_up(size + shift, STRIPE)
            host = PLACED_ON.get(name)
            if name in SAME_BYTES:
                start = extent[SAME_BYTES[name]][0]
            elif host is None:
                room = ROOM if name in spent else 0
                start = cursor["fresh"] + room
                cursor["fresh"] = start + length + room
            else:
                begin, end = extent[host]
                placed[host] = placed.get(host, 0) + 1
                if host not in PLACED_ON and placed[host] == 1:
                    start = begin + STRIPE - length
                elif host not in PLACED_ON and placed[host] == 2:
                    start = end - STRIPE
                else:
                    start = cursor.get(host, begin if host in PLACED_ON else begin + STRIPE)
                    cursor[host] = start + length
                    assert start + shift < end, name
            extent[name] = (start, start + length)
            return work.tile(shape, dtype, name=name, align_bytes=SHIFT if moving else STRIPE, offset=start + shift)

        offsets = keep.tile([P, J // PER_COLUMN], U16, name="offsets")
        tab_plane = sb([P, T], U8, "tab_plane")
        wx_plane = sb([P, N], U8, "wx_plane")
        wx_codes = sb([P, 2 * N], U8, "wx_codes")
        ramp = sb([P, KP // 2], BF16, "ramp")
        eye = sb([P, PACK * KP], BF16, "eye")
        eye_codes = sb([P, KP], U32, "eye_codes")
        eye_plane = sb([P, KP], U8, "eye_plane")
        w_raw, w_bf, tab_raw, x_raw, x_bf = {}, {}, {}, {}, {}
        first, second, rest, back, words, scales, xq = {}, {}, {}, {}, {}, {}, {}
        sums, passes_left, results = {}, {}, {}

        def listed(j0, j1):
            return offsets[:, j0 // PER_COLUMN : j1 // PER_COLUMN]

        def load_w(a, chunks):
            raw = sb([P, PACK, CHUNK * len(chunks)], F32, f"w_raw{a}{chunks[0]}")
            cols = slice(CHUNK * chunks[0], CHUNK * (chunks[-1] + 1))
            nc.sync.dma_start(raw[:], wt[KP * a : KP * (a + 1), cols].rearrange("(p t) n -> p t n", t=PACK))
            for c in chunks:
                w_raw[a, c] = (raw, CHUNK * (c - chunks[0]))

        def raw_columns(a, chunks):
            raw, at = w_raw[a, chunks[0]]
            return raw[:, :, at : at + CHUNK * len(chunks)]

        def load_table(a):
            tab_raw[a] = sb([P, T], I32, f"tab_raw{a}")
            nc.sync.dma_start(tab_raw[a][:], tab_words[a].rearrange("p c t -> p (c t)").bitcast(I32))

        def load_table_scales(queue, q):
            rows = tab_plane[QUADRANT * q : QUADRANT * q + 2 * PACK, :]
            queue.dma_start(rows.bitcast(I32), tab_scales[:, PACK * q : PACK * (q + 1), :].bitcast(I32))

        def load_wx_scales():
            for q in range(4):
                rows = wx_plane[QUADRANT * q : QUADRANT * q + PACK, :]
                nc.sync.dma_start(rows.bitcast(I32), wx_scales[0, PACK * q : PACK * (q + 1), :].bitcast(I32))

        def load_wx_words():
            nc.sync.dma_start(wx_codes[:].bitcast(I32), wx_words[0].bitcast(I32))

        def load_x(s):
            x_raw[s] = sb([P, PACK, QUARTER], F32, f"x_raw{s}")
            nc.sync.dma_start(x_raw[s][:], x[:, QUARTER * s : QUARTER * (s + 1)].rearrange("(p t) j -> p t j", t=PACK))

        def make_ramp():
            nc.gpsimd.iota(ramp[:], pattern=[[1, KP // 2]], base=P, channel_multiplier=-PACK, allow_small_or_imprecise_dtypes=True)

        def make_identity():
            for t in range(PACK):
                for h in range(2):
                    at = KP * t + KP // 2 * h
                    nc.vector.tensor_scalar(
                        out=eye[:, at : at + KP // 2], in0=ramp[:], scalar1=float(P + t - KP // 2 * h), scalar2=None, op0=mybir.AluOpType.is_equal
                    )
            for h in range(2):
                cols = slice(KP // 2 * h, KP // 2 * (h + 1))
                nc.vector.quantize_mx(out=eye_codes[:, cols].bitcast(FP8X4), scales=eye_plane[:, cols], in_=eye[:, 2 * KP * h : 2 * KP * (h + 1)])

        def gather_scales(j0, j1):
            base = 0 if j0 < SPANS["C"][0] else SPANS["C"][0]
            if base not in scales:
                scales[base] = sb([P, SPANS["C"][0] if base == 0 else QUARTER], U8, f"scales{base}")
            nc.vector.tensor_copy(scales[base][:, j0 - base : j1 - base], tab_plane[:].indirect(listed(j0, j1)))

        def gather_words(a, span):
            j0, j1 = SPANS[span]
            words[a, span] = sb([P, j1 - j0], U32, f"words{a}{span}", moving=True)
            nc.vector.tensor_copy(words[a, span][:], tab_raw[a][:].bitcast(U32).indirect(listed(j0, j1)))

        def quantize(codes, plane, grouped):
            nc.vector.quantize_mx(out=codes.bitcast(FP8X4), scales=plane, in_=grouped[:].rearrange("p c t -> p (c t)"))

        def quantize_weights(tier, name, a, chunks, grouped):
            codes = sb([P, CHUNK * len(chunks)], U32, f"{name}{a}{chunks[0]}_codes")
            plane = sb([P, CHUNK * len(chunks)], U8, f"{name}{a}{chunks[0]}_plane")
            quantize(codes[:], plane[:], grouped)
            for i, c in enumerate(chunks):
                cols = slice(CHUNK * i, CHUNK * (i + 1))
                tier[a, c] = (codes[:, cols].bitcast(FP8X4), plane[:, cols])

        def cast_w(a, chunks):
            w_bf[a, chunks] = sb([P, CHUNK * len(chunks), PACK], BF16, f"w_bf{a}{chunks[0]}")
            nc.scalar.copy(out=woven(w_bf[a, chunks][:]), in_=by_rows(raw_columns(a, chunks)))

        def first_tier(a, chunks):
            quantize_weights(first, "wq", a, chunks, w_bf[a, chunks])

        def read_back(a, c):
            codes, plane = first[a, c]
            back[a, c] = psum.tile([P, PACK, CHUNK], F32, name="back", tag=f"back{c % 2}")
            for t in range(PACK):
                cols = slice(P * t, P * (t + 1))
                nc.tensor.matmul_mx(
                    out=back[a, c][:, t, :], lhsT=eye_codes[:, cols].bitcast(FP8X4), lhsT_scale=eye_plane[:, cols], rhs=codes, rhs_scale=plane, start=True, stop=True
                )

        def subtract(a, c, chunks):
            if (a, chunks) not in rest:
                rest[a, chunks] = sb([P, CHUNK * len(chunks), PACK], BF16, f"rest{a}{chunks[0]}")
            at = CHUNK * chunks.index(c)
            nc.vector.tensor_tensor(
                out=woven(rest[a, chunks][:, at : at + CHUNK, :]), in0=by_rows(raw_columns(a, (c,))), in1=by_rows(back[a, c][:]), op=mybir.AluOpType.subtract
            )

        def second_tier(a, chunks):
            quantize_weights(second, "wr", a, chunks, rest[a, chunks])

        def cast_x(j0, j1, engine_copy):
            x_bf[j0] = sb([P, j1 - j0, PACK], BF16, f"x_bf{j0}")
            s = j0 // QUARTER
            engine_copy(out=woven(x_bf[j0][:]), in_=by_rows(x_raw[s][:, :, j0 - QUARTER * s : j1 - QUARTER * s]))

        def quantize_x(j0, j1):
            s = j0 // QUARTER
            if s not in xq:
                xq[s] = (sb([P, QUARTER], U32, f"xq{s}_codes", moving=True), sb([P, QUARTER], U8, f"xq{s}_plane"))
            codes, plane = xq[s]
            cols = slice(j0 - QUARTER * s, j1 - QUARTER * s)
            quantize(codes[:, cols], plane[:, cols], x_bf[j0])

        def add_pass(c, span, j0, j1, lhsT, lhsT_scale, rhs, rhs_scale):
            name, bank, at, chunks_in_bank = SUMS[span][c]
            base, end = SPANS[span]
            count = (4 + (end - base) // QUARTER) * chunks_in_bank
            if name not in sums:
                sums[name] = psum.tile([P, BANK], F32, name=name, tag=bank)
                passes_left[name] = count
            nc.tensor.matmul_mx(
                out=sums[name][:, at + j0 - base : at + j1 - base],
                lhsT=lhsT,
                lhsT_scale=lhsT_scale,
                rhs=rhs,
                rhs_scale=rhs_scale,
                start=(passes_left[name] == count),
                stop=(passes_left[name] == 1),
            )
            passes_left[name] = passes_left[name] - 1

        def table_passes(tier, a, chunks, span):
            j0, j1 = SPANS[span]
            base = max(b for b in scales if b <= j0)
            for c in chunks:
                codes, plane = tier[a, c]
                add_pass(c, span, j0, j1, codes, plane, words[a, span][:].bitcast(FP8X4), scales[base][PACK * a : P, j0 - base : j1 - base])

        def both_tiers(a, c, span):
            table_passes(first, a, (c,), span)
            table_passes(second, a, (c,), span)

        def x_passes(chunks, s):
            codes, plane = xq[s]
            for c in chunks:
                stationary = wx_codes[:, 2 * CHUNK * c : 2 * CHUNK * (c + 1)].bitcast(FP4X4)
                scale = wx_plane[:, CHUNK * c : CHUNK * (c + 1)]
                add_pass(c, "AABC"[s], QUARTER * s, QUARTER * (s + 1), stationary, scale, codes[:].bitcast(FP8X4), plane[:])

        def store(c, span, engine_copy):
            name, bank, at, count = SUMS[span][c]
            j0, j1 = SPANS[span]
            result = sb([P, count, j1 - j0], F32, f"result{c}{span}")
            results[c, span] = result
            engine_copy(out=result[:].rearrange("p c j -> p (c j)"), in_=sums[name][:, 0 : count * (j1 - j0)])
            rows = out[CHUNK * c : CHUNK * (c + count), j0:j1].rearrange("(c p) j -> p c j", p=P)
            nc.sync.dma_start(rows, result[:])

        on_scalar, on_vector = nc.scalar.copy, nc.vector.tensor_copy

        nc.vector.memset(tab_plane[:].bitcast(I32), 0)
        load_w(0, LOW)
        nc.sync.dma_start(offsets[:], offs)
        for q in range(4):
            load_table_scales(nc.sync, q)
        nc.vector.memset(wx_plane[:].bitcast(I32), 0)
        make_ramp()
        make_identity()
        load_w(0, HIGH)
        load_table(0)
        load_w(1, LOW)
        load_w(1, HIGH)
        load_table(1)
        load_wx_scales()
        load_x(0)
        load_wx_words()
        for s in range(1, 4):
            load_x(s)
        for a in range(2):
            cast_w(a, LOW)
            cast_w(a, HIGH)
        for s in range(3):
            cast_x(QUARTER * s, QUARTER * (s + 1), on_scalar)

        gather_scales(0, 256)
        first_tier(0, LOW)
        read_back(0, 0)
        read_back(0, 1)
        gather_scales(256, 768)
        subtract(0, 0, LOW)
        first_tier(0, HIGH)
        read_back(0, 2)
        subtract(0, 1, LOW)
        read_back(0, 3)
        gather_words(0, "B")
        table_passes(first, 0, ALL, "B")
        second_tier(0, LOW)
        table_passes(second, 0, LOW, "B")
        gather_words(0, "A")
        table_passes(first, 0, ALL, "A")
        subtract(0, 2, HIGH)
        subtract(0, 3, HIGH)
        first_tier(1, LOW)
        table_passes(second, 0, LOW, "A")
        read_back(1, 0)
        read_back(1, 1)
        first_tier(1, HIGH)
        second_tier(0, HIGH)
        for span in "AB":
            table_passes(second, 0, HIGH, span)

        gather_words(1, "A")
        table_passes(first, 1, LOW, "A")
        subtract(1, 0, LOW)
        table_passes(first, 1, (2,), "A")
        read_back(1, 2)
        table_passes(first, 1, (3,), "A")
        subtract(1, 1, LOW)
        read_back(1, 3)
        gather_words(1, "B")
        table_passes(first, 1, ALL, "B")
        second_tier(1, LOW)
        for span in "AB":
            table_passes(second, 1, LOW, span)
        quantize_x(0, 256)
        x_passes(ALL, 0)
        subtract(1, 2, (2,))
        quantize_x(256, 512)
        x_passes(ALL, 1)
        store(0, "A", on_scalar)
        store(1, "A", on_scalar)
        second_tier(1, (2,))
        table_passes(second, 1, (2,), "A")
        store(2, "A", on_scalar)
        subtract(1, 3, (3,))
        gather_scales(768, 1024)
        second_tier(1, (3,))
        table_passes(second, 1, (3,), "A")
        store(3, "A", on_scalar)
        table_passes(second, 1, HIGH, "B")
        quantize_x(512, 768)
        x_passes(ALL, 2)
        store(0, "B", on_scalar)
        store(2, "B", on_scalar)
        gather_words(0, "C")

        for c in LOW:
            both_tiers(0, c, "C")
        gather_words(1, "C")
        for c in LOW:
            both_tiers(1, c, "C")
        for a in range(2):
            both_tiers(a, 2, "C")
        cast_x(768, 896, on_vector)
        cast_x(896, 1024, on_vector)
        quantize_x(768, 896)
        quantize_x(896, 1024)
        for c in range(3):
            x_passes((c,), 3)
            store(c, "C", on_vector if c == 1 else on_scalar)
        for a in range(2):
            both_tiers(a, 3, "C")
        x_passes((3,), 3)
        store(3, "C", on_vector)
